import numpy as np
import ml_dtypes


def mxq(x, axis, fmt="e4m3"):
    dtype, down = {"e4m3": (ml_dtypes.float8_e4m3fn, 7), "e5m2": (ml_dtypes.float8_e5m2, 14)}[fmt]
    v = np.moveaxis(np.asarray(x, np.float32).astype(ml_dtypes.bfloat16).astype(np.float64), axis, -1)
    blocks = v.reshape(v.shape[:-1] + (-1, 32))
    amax = np.abs(blocks).max(-1, keepdims=True)
    byte = np.maximum(np.where(amax > 0, np.frexp(amax)[1] - 1 + 127, 0) - down, 1)
    scale = np.exp2(byte - 127.0)
    codes = (blocks / scale).astype(np.float32).astype(dtype).astype(np.float64)
    return np.moveaxis((codes * scale).reshape(v.shape), -1, axis)


WIDE = False


def mx_kscale(k):
    if not WIDE:
        return np.ones(k)
    levels = np.array([24, -24, 12, -12, 0])
    if k % 512:
        return np.exp2(np.random.permutation(np.resize(levels, k // 32))).repeat(32)
    a = np.empty((k // 512, 16))
    for p in range(k // 512):
        a[p, :8] = np.random.permutation(np.resize(levels, 8))
        for g in range(8):
            far = levels[np.abs(levels - a[p, g]) >= 10]
            a[p, g + 8] = far[np.random.randint(len(far))]
    return np.exp2(a.ravel()).repeat(32)


def f64(x):
    return np.asarray(x).astype(np.float64)


def striped(idx):
    return np.tile(idx.reshape(-1, 16).T, (8, 1)).astype(np.uint16)


def unstriped(offs):
    return offs[:16].T.reshape(-1).astype(np.int64)


E2M1 = np.array([0.0, 0.5, 1.0, 1.5, 2.0, 3.0, 4.0, 6.0, -0.0, -0.5, -1.0, -1.5, -2.0, -3.0, -4.0, -6.0])


def pack_weight(w, fmt):
    k, n = w.shape
    w = f64(np.asarray(w, np.float32).astype(ml_dtypes.bfloat16)).reshape(k // 32, 32, n)
    amax = np.abs(w).max(1)
    if fmt == "e4m3":
        byte = np.frexp(amax)[1] - 1 + 127 - 7
    else:
        mant, ex = np.frexp(amax / 6.0)
        byte = np.where(mant > 0.5, ex, ex - 1) + 127
    byte = np.clip(np.where(amax > 0, byte, 1), 1, 254)
    scaled = (w * np.exp2(127.0 - byte)[:, None, :]).reshape(k, n).astype(np.float32)
    by_word = np.ascontiguousarray(scaled.reshape(k // 512, 128, 4, n).transpose(0, 1, 3, 2))
    if fmt == "e4m3":
        words = by_word.astype(ml_dtypes.float8_e4m3fn).view(np.uint8)
    else:
        c = by_word.astype(ml_dtypes.float4_e2m1fn).view(np.uint8) & 0xF
        words = (c[..., 0::2] | (c[..., 1::2] << 4)).reshape(k // 512, 128, 2 * n)
    return np.ascontiguousarray(words), np.ascontiguousarray(byte.astype(np.uint8).reshape(k // 512, 16, n))


def unpack_weight(words, scales, fmt):
    g, _, n = scales.shape
    words = np.ascontiguousarray(words).reshape(g, 128, n, -1)
    if fmt == "e4m3":
        vals = words.view(ml_dtypes.float8_e4m3fn).astype(np.float64)
    else:
        nib = np.empty((g, 128, n, 4), np.uint8)
        nib[..., 0::2] = words & 0xF
        nib[..., 1::2] = words >> 4
        vals = E2M1[nib]
    vals = vals * np.repeat(np.exp2(scales.astype(np.float64) - 127.0), 8, axis=1)[..., None]
    return vals.transpose(0, 1, 3, 2).reshape(g * 512, n)


def pack_table4(v):
    words, scales = pack_weight(v, "e2m1")
    g, t = words.shape[0] // 2, v.shape[1]
    return np.ascontiguousarray(words.reshape(g, 2, 128, t, 2).transpose(0, 2, 3, 1, 4).reshape(g, 128, t, 4)), scales


def unpack_table4(words, scales):
    g, _, t, _ = words.shape
    return unpack_weight(words.reshape(g, 128, t, 2, 2).transpose(0, 3, 1, 2, 4).reshape(2 * g, 128, 2 * t), scales, "e2m1")


K, R, N, T, J = 1024, 512, 256, 2048, 1024


def setup_inputs():
    n = np.random.standard_normal
    s = mx_kscale(K)[:, None]
    u = mx_kscale(R)[:, None]
    wd = n((R, N)) / np.sqrt(R) / u
    wd4 = pack_weight(wd, "e2m1")
    wdrest = wd - unpack_weight(*wd4, "e2m1")
    p_tab = pack_table4(n((K, T)) * s)
    p_wd8 = pack_weight(wdrest, "e4m3")
    return {
        "tab_words": p_tab[0],
        "tab_scales": p_tab[1],
        "wg": (n((K, R)) / np.sqrt(K) / s).astype(np.float32),
        "wu": (n((K, R)) / np.sqrt(K) / s * u.T).astype(np.float32),
        "wd4_words": wd4[0],
        "wd4_scales": wd4[1],
        "wd8_words": p_wd8[0],
        "wd8_scales": p_wd8[1],
        "offs": striped(np.random.permutation(T)[:J]),
    }


def reference(tab_words, tab_scales, wg, wu, wd4_words, wd4_scales, wd8_words, wd8_scales, offs):
    idx = unstriped(offs)
    tab_ = unpack_table4(tab_words, tab_scales)[:, idx]
    wg_ = mxq(f64(wg), 0, "e4m3")
    wu_ = mxq(f64(wu), 0, "e4m3")
    ga = wg_.T @ tab_
    ub = wu_.T @ tab_
    h = np.tanh(ga) * ub
    h_ = mxq(h, 0, "e4m3")
    wd4_ = unpack_weight(wd4_words, wd4_scales, "e2m1")
    wd8_ = unpack_weight(wd8_words, wd8_scales, "e4m3")
    y = wd4_.T @ h_ + wd8_.T @ h_
    return y

@@ -1,0 +1,242 @@
+from contextlib import ExitStack
+
+import concourse.mybir as mybir
+
+K, R, N, T, J = 1024, 512, 256, 2048, 1024
+FLOPS = 2 * J * (2 * K * R + 2 * R * N)
+
+F32 = mybir.dt.float32
+BF16 = mybir.dt.bfloat16
+I32 = mybir.dt.int32
+U32 = mybir.dt.uint32
+U16 = mybir.dt.uint16
+U8 = mybir.dt.uint8
+FP8X4 = mybir.dt.float8_e4m3fn_x4
+FP4X4 = mybir.dt.float4_e2m1fn_x4
+TANH = mybir.ActivationFunctionType.Tanh
+MULT = mybir.AluOpType.mult
+
+P = 128
+PACK = 4
+K_PASS = P * PACK
+PASSES = K // K_PASS
+HALF = 512
+CHUNK = 128
+SHIFT = 16
+
+
+def tile_list_gmlpt_tanh_res_none_kernel(
+    tc, tab_words, tab_scales, wg, wu, wd4_words, wd4_scales, wd8_words, wd8_scales, offs, out
+):
+    nc = tc.nc
+    with ExitStack() as ctx:
+        keep = ctx.enter_context(tc.tile_pool(name="keep", bufs=1))
+        psum = ctx.enter_context(tc.psum_pool(name="psum", bufs=8))
+
+        offsets = keep.tile([P, J // 16], U16, name="offsets")
+        scale_window = keep.tile([P, T // 4], I32, name="scale_window", align_bytes=64)
+        word_window = keep.tile([P, T], I32, name="word_window", align_bytes=64)
+        picked_scales = keep.tile([P, J // 4], I32, name="picked_scales", align_bytes=64)
+        moved_scales = keep.tile([P, J // 4], I32, name="moved_scales", align_bytes=64)
+        picked_words = keep.tile([P, J], I32, name="picked_words", align_bytes=64)
+        v_codes = keep.tile([P, PASSES, 2 * J], U8, name="v_codes", align_bytes=64)
+        wd4_codes = keep.tile([P, 2 * N // 4], I32, name="wd4_codes", align_bytes=64)
+        wd8_codes = keep.tile([P, N], I32, name="wd8_codes", align_bytes=64)
+        wd_scales = keep.tile([P, 2, N // 4], I32, name="wd_scales", align_bytes=64)
+        warm = keep.tile([P, 8], F32, name="warm")
+        warm_out = keep.tile([P, 8], F32, name="warm_out")
+
+        nc.gpsimd.memset(scale_window[:], 0)
+        nc.vector.memset(warm[:], 0.0)
+        nc.gpsimd.memset(moved_scales[:], 0)
+        nc.gpsimd.memset(wd_scales[:], 0)
+
+        nc.sync.dma_start(offsets[:], offs)
+        nc.sync.dma_start(word_window[:], tab_words[0].rearrange("p t b -> p (t b)").bitcast(I32))
+        scale_rows = tab_scales.bitcast(I32).rearrange("a (q r) t -> r q a t", r=4)
+        for r in range(4):
+            nc.sync.dma_start(scale_window[r:P:SHIFT, :], scale_rows[r])
+        nc.scalar.activation(warm_out[:], warm[:], TANH)
+
+        raw = {}
+        for name, w in (("g", wg), ("u", wu)):
+            for a in range(PASSES):
+                raw[name, a] = keep.tile([P, PACK, R], F32, name="raw_%s%d" % (name, a))
+                nc.sync.dma_start(
+                    raw[name, a][:], w[a * K_PASS : (a + 1) * K_PASS, :].rearrange("(p j) c -> p j c", j=PACK)
+                )
+        nc.sync.dma_start(wd4_codes[:], wd4_words[0].bitcast(I32))
+        nc.sync.dma_start(wd8_codes[:], wd8_words[0].rearrange("p n b -> p (n b)").bitcast(I32))
+        for f, scales in enumerate((wd4_scales, wd8_scales)):
+            rows = scales[0].bitcast(I32).rearrange("(q r) n -> r q n", r=4)
+            for r in range(4):
+                nc.sync.dma_start(wd_scales[r:P:32, f, :], rows[r])
+
+        grouped, w_codes, w_scales = {}, {}, {}
+        for key in raw:
+            grouped[key] = keep.tile([P, PACK, P * PACK], BF16, name="grouped_%s%d" % key, align_bytes=64)
+            w_codes[key] = keep.tile([P, R], U32, name="w_codes_%s%d" % key, align_bytes=64)
+            w_scales[key] = keep.tile([P, R], U8, name="w_scales_%s%d" % key, align_bytes=64)
+
+        def cast(key, u, copy):
+            src = raw[key][:].rearrange("p j (m u e) -> p u m j e", u=2, e=2)[:, u]
+            dst = grouped[key][:, 2 * u : 2 * u + 2, :].rearrange("p e (m j) -> p m j e", j=PACK)
+            copy(dst, src)
+
+        def quantize_weight(key, u):
+            cols = slice(2 * u * P, 2 * (u + 1) * P)
+            nc.vector.quantize_mx(
+                out=w_codes[key][:, cols].bitcast(FP8X4),
+                scales=w_scales[key][:, cols],
+                in_=grouped[key][:, 2 * u : 2 * u + 2, :].rearrange("p e x -> p (e x)"),
+            )
+
+        def gather_words(h):
+            nc.vector.tensor_copy(
+                picked_words[:, h * HALF : (h + 1) * HALF].bitcast(U32),
+                word_window[:].bitcast(U32).indirect(offsets[:, h * HALF // 16 : (h + 1) * HALF // 16]),
+            )
+
+        def gather_scales(h):
+            nc.vector.tensor_copy(
+                picked_scales[:].bitcast(U8)[:, h * HALF : (h + 1) * HALF],
+                scale_window[:].bitcast(U8).indirect(offsets[:, h * HALF // 16 : (h + 1) * HALF // 16]),
+            )
+            words = slice(h * HALF // 4, (h + 1) * HALF // 4)
+            nc.gpsimd.dma_start(moved_scales[0 : P - SHIFT, words], picked_scales[SHIFT:P, words])
+
+        def part_words(h):
+            src = picked_words[:, h * HALF : (h + 1) * HALF].bitcast(U16).rearrange("p (j d) -> p d j", d=2)
+            dst = v_codes[:, :, 2 * h * HALF : 2 * (h + 1) * HALF].bitcast(U16)
+            nc.vector.tensor_copy(dst, src)
+
+        v_scales = (picked_scales[:].bitcast(U8), moved_scales[:].bitcast(U8))
+
+        def first_layer_pass(acc, key, t, j0, width):
+            a = key[1]
+            nc.tensor.matmul_mx(
+                out=acc,
+                lhsT=w_codes[key][:, t * P : (t + 1) * P].bitcast(FP8X4),
+                lhsT_scale=w_scales[key][:, t * P : (t + 1) * P],
+                rhs=v_codes[:, a, 2 * j0 : 2 * (j0 + width)].bitcast(FP4X4),
+                rhs_scale=v_scales[a][:, j0 : j0 + width],
+                start=(a == 0),
+                stop=(a == PASSES - 1),
+            )
+
+        gather_words(0)
+        gather_scales(0)
+        part_words(0)
+        cast(("g", 0), 0, nc.scalar.copy)
+        cast(("g", 0), 1, nc.scalar.copy)
+        quantize_weight(("g", 0), 0)
+        gather_words(1)
+        quantize_weight(("g", 0), 1)
+        gather_scales(1)
+        part_words(1)
+        cast(("g", 1), 0, nc.scalar.copy)
+        cast(("g", 1), 1, nc.scalar.copy)
+        quantize_weight(("g", 1), 0)
+        quantize_weight(("g", 1), 1)
+        cast(("u", 0), 0, nc.scalar.copy)
+        cast(("u", 0), 1, nc.vector.tensor_copy)
+        quantize_weight(("u", 0), 0)
+        cast(("u", 1), 0, nc.vector.tensor_copy)
+        quantize_weight(("u", 0), 1)
+        cast(("u", 1), 1, nc.vector.tensor_copy)
+        quantize_weight(("u", 1), 0)
+        quantize_weight(("u", 1), 1)
+
+        gate_banks = {}
+        for h in range(2):
+            for t in range(PACK):
+                gate_banks[h, t] = psum.tile([P, HALF], F32, name="bank")
+                first_layer_pass(gate_banks[h, t][:], ("g", 0), t, h * HALF, HALF)
+        gate = keep.tile([P, PACK, J], F32, name="gate")
+        for h in range(2):
+            for t in range(PACK):
+                first_layer_pass(gate_banks[h, t][:], ("g", 1), t, h * HALF, HALF)
+                nc.scalar.activation(gate[:, t, h * HALF : (h + 1) * HALF], gate_banks[h, t][:], TANH)
+
+        hidden = keep.tile([P, J * PACK], BF16, name="hidden", align_bytes=64)
+        h_codes = keep.tile([P, J], U32, name="h_codes", align_bytes=64)
+        h_scales = keep.tile([P, J], U8, name="h_scales", align_bytes=64)
+        result = keep.tile([P, N // P, J], F32, name="result")
+        out_rows = out.rearrange("(b p) j -> p b j", p=P)
+        wd_planes = wd_scales[:].bitcast(U8)
+
+        def up_and_multiply(c):
+            j0 = c * CHUNK
+            bank = psum.tile([P, HALF], F32, name="bank")
+            for t in range(PACK):
+                for a in range(PASSES):
+                    first_layer_pass(bank[:, t * CHUNK : (t + 1) * CHUNK], ("u", a), t, j0, CHUNK)
+            nc.vector.tensor_tensor(
+                hidden[:, j0 * PACK : (j0 + CHUNK) * PACK].rearrange("p (c e t) -> p c t e", e=2, t=PACK),
+                bank[:].rearrange("p (t c e) -> p c t e", t=PACK, e=2),
+                gate[:, :, j0 : j0 + CHUNK].rearrange("p t (c e) -> p c t e", e=2),
+                MULT,
+            )
+
+        def quantize_hidden(j0, width):
+            nc.vector.quantize_mx(
+                out=h_codes[:, j0 : j0 + width].bitcast(FP8X4),
+                scales=h_scales[:, j0 : j0 + width],
+                in_=hidden[:, j0 * PACK : (j0 + width) * PACK],
+            )
+
+        def down_group(acc, b, j0, width):
+            moving = dict(rhs=h_codes[:, j0 : j0 + width].bitcast(FP8X4), rhs_scale=h_scales[:, j0 : j0 + width])
+            nc.tensor.matmul_mx(
+                out=acc,
+                lhsT=wd4_codes[:].bitcast(U8)[:, 2 * b * P : 2 * (b + 1) * P].bitcast(FP4X4),
+                lhsT_scale=wd_planes[:, 0, b * P : (b + 1) * P],
+                start=True,
+                stop=False,
+                **moving
+            )
+            nc.tensor.matmul_mx(
+                out=acc,
+                lhsT=wd8_codes[:, b * P : (b + 1) * P].bitcast(FP8X4),
+                lhsT_scale=wd_planes[:, 1, b * P : (b + 1) * P],
+                start=False,
+                stop=True,
+                **moving
+            )
+
+        def down_wide(j0):
+            for b in range(N // P):
+                bank = psum.tile([P, HALF], F32, name="bank")
+                down_group(bank[:], b, j0, HALF)
+                nc.scalar.copy(result[:, b, j0 : j0 + HALF], bank[:])
+                nc.sync.dma_start(out_rows[:, b, j0 : j0 + HALF], result[:, b, j0 : j0 + HALF])
+
+        def down_narrow(c):
+            j0 = c * CHUNK
+            bank = psum.tile([P, HALF], F32, name="bank")
+            for b in range(N // P):
+                down_group(bank[:, b * CHUNK : (b + 1) * CHUNK], b, j0, CHUNK)
+            nc.scalar.copy(
+                result[:, :, j0 : j0 + CHUNK], bank[:, 0 : 2 * CHUNK].rearrange("p (b j) -> p b j", b=N // P)
+            )
+            nc.sync.dma_start(out_rows[:, :, j0 : j0 + CHUNK], result[:, :, j0 : j0 + CHUNK])
+
+        up_and_multiply(0)
+        up_and_multiply(1)
+        up_and_multiply(2)
+        quantize_hidden(0, 2 * CHUNK)
+        up_and_multiply(3)
+        up_and_multiply(4)
+        quantize_hidden(2 * CHUNK, 2 * CHUNK)
+        up_and_multiply(5)
+        quantize_hidden(4 * CHUNK, CHUNK)
+        down_wide(0)
+        up_and_multiply(6)
+        quantize_hidden(5 * CHUNK, CHUNK)
+        up_and_multiply(7)
+        quantize_hidden(6 * CHUNK, CHUNK)
+        down_narrow(4)
+        down_narrow(5)
+        quantize_hidden(7 * CHUNK, CHUNK)
+        down_narrow(6)
+        down_narrow(7)

@@ -52,10 +52,12 @@ def tile_list_gmlpt_tanh_res_none_kernel(
         nc.gpsimd.memset(wd_scales[:], 0)
 
         nc.sync.dma_start(offsets[:], offs)
-        nc.sync.dma_start(word_window[:], tab_words[0].rearrange("p t b -> p (t b)").bitcast(I32))
+        table_words = tab_words[0].rearrange("p t b -> p (t b)").bitcast(I32)
+        nc.sync.dma_start(word_window[:, 0 : T // 2], table_words[:, 0 : T // 2])
         scale_rows = tab_scales.bitcast(I32).rearrange("a (q r) t -> r q a t", r=4)
         for r in range(4):
             nc.sync.dma_start(scale_window[r:P:SHIFT, :], scale_rows[r])
+        nc.sync.dma_start(word_window[:, T // 2 : T], table_words[:, T // 2 : T])
         nc.scalar.activation(warm_out[:], warm[:], TANH)
 
         raw = {}
@@ -72,15 +74,15 @@ def tile_list_gmlpt_tanh_res_none_kernel(
             for r in range(4):
                 nc.sync.dma_start(wd_scales[r:P:32, f, :], rows[r])
 
-        grouped, w_codes, w_scales = {}, {}, {}
+        grouped = [keep.tile([P, 2, P * PACK], BF16, name="grouped%d" % u, align_bytes=64) for u in range(2)]
+        w_codes, w_scales = {}, {}
         for key in raw:
-            grouped[key] = keep.tile([P, PACK, P * PACK], BF16, name="grouped_%s%d" % key, align_bytes=64)
             w_codes[key] = keep.tile([P, R], U32, name="w_codes_%s%d" % key, align_bytes=64)
             w_scales[key] = keep.tile([P, R], U8, name="w_scales_%s%d" % key, align_bytes=64)
 
         def cast(key, u, copy):
             src = raw[key][:].rearrange("p j (m u e) -> p u m j e", u=2, e=2)[:, u]
-            dst = grouped[key][:, 2 * u : 2 * u + 2, :].rearrange("p e (m j) -> p m j e", j=PACK)
+            dst = grouped[u][:].rearrange("p e (m j) -> p m j e", j=PACK)
             copy(dst, src)
 
         def quantize_weight(key, u):
@@ -88,7 +90,7 @@ def tile_list_gmlpt_tanh_res_none_kernel(
             nc.vector.quantize_mx(
                 out=w_codes[key][:, cols].bitcast(FP8X4),
                 scales=w_scales[key][:, cols],
-                in_=grouped[key][:, 2 * u : 2 * u + 2, :].rearrange("p e x -> p (e x)"),
+                in_=grouped[u][:].rearrange("p e x -> p (e x)"),
             )
 
         def gather_words(h):
@@ -96,14 +98,6 @@ def tile_list_gmlpt_tanh_res_none_kernel(
                 picked_words[:, h * HALF : (h + 1) * HALF].bitcast(U32),
                 word_window[:].bitcast(U32).indirect(offsets[:, h * HALF // 16 : (h + 1) * HALF // 16]),
             )
-
-        def gather_scales(h):
-            nc.vector.tensor_copy(
-                picked_scales[:].bitcast(U8)[:, h * HALF : (h + 1) * HALF],
-                scale_window[:].bitcast(U8).indirect(offsets[:, h * HALF // 16 : (h + 1) * HALF // 16]),
-            )
-            words = slice(h * HALF // 4, (h + 1) * HALF // 4)
-            nc.gpsimd.dma_start(moved_scales[0 : P - SHIFT, words], picked_scales[SHIFT:P, words])
 
         def part_words(h):
             src = picked_words[:, h * HALF : (h + 1) * HALF].bitcast(U16).rearrange("p (j d) -> p d j", d=2)
@@ -124,21 +118,21 @@ def tile_list_gmlpt_tanh_res_none_kernel(
                 stop=(a == PASSES - 1),
             )
 
+        nc.vector.tensor_copy(picked_scales[:].bitcast(U8), scale_window[:].bitcast(U8).indirect(offsets[:]))
+        nc.gpsimd.dma_start(moved_scales[0 : P - SHIFT, :], picked_scales[SHIFT:P, :])
         gather_words(0)
-        gather_scales(0)
+        gather_words(1)
         part_words(0)
+        part_words(1)
         cast(("g", 0), 0, nc.scalar.copy)
         cast(("g", 0), 1, nc.scalar.copy)
         quantize_weight(("g", 0), 0)
-        gather_words(1)
-        quantize_weight(("g", 0), 1)
-        gather_scales(1)
-        part_words(1)
         cast(("g", 1), 0, nc.scalar.copy)
+        quantize_weight(("g", 0), 1)
         cast(("g", 1), 1, nc.scalar.copy)
         quantize_weight(("g", 1), 0)
-        quantize_weight(("g", 1), 1)
         cast(("u", 0), 0, nc.scalar.copy)
+        quantize_weight(("g", 1), 1)
         cast(("u", 0), 1, nc.vector.tensor_copy)
         quantize_weight(("u", 0), 0)
         cast(("u", 1), 0, nc.vector.tensor_copy)
@@ -230,13 +224,13 @@ def tile_list_gmlpt_tanh_res_none_kernel(
         quantize_hidden(2 * CHUNK, 2 * CHUNK)
         up_and_multiply(5)
         quantize_hidden(4 * CHUNK, CHUNK)
-        down_wide(0)
         up_and_multiply(6)
         quantize_hidden(5 * CHUNK, CHUNK)
         up_and_multiply(7)
         quantize_hidden(6 * CHUNK, CHUNK)
+        quantize_hidden(7 * CHUNK, CHUNK)
+        down_wide(0)
         down_narrow(4)
         down_narrow(5)
-        quantize_hidden(7 * CHUNK, CHUNK)
         down_narrow(6)
         down_narrow(7)

@@ -23,6 +23,9 @@ PASSES = K // K_PASS
 HALF = 512
 CHUNK = 128
 SHIFT = 16
+GATE_BANKS = ((0, 1, 2, 3), (4, 5, 0, 1))
+UP_BANKS = (6, 7, 2, 3)
+LAST_PIECES = ((0, 384), (384, R))
 
 
 def tile_list_gmlpt_tanh_res_none_kernel(
@@ -31,7 +34,7 @@ def tile_list_gmlpt_tanh_res_none_kernel(
     nc = tc.nc
     with ExitStack() as ctx:
         keep = ctx.enter_context(tc.tile_pool(name="keep", bufs=1))
-        psum = ctx.enter_context(tc.psum_pool(name="psum", bufs=8))
+        psum = ctx.enter_context(tc.psum_pool(name="psum", bufs=1))
 
         offsets = keep.tile([P, J // 16], U16, name="offsets")
         scale_window = keep.tile([P, T // 4], I32, name="scale_window", align_bytes=64)
@@ -39,7 +42,6 @@ def tile_list_gmlpt_tanh_res_none_kernel(
         picked_scales = keep.tile([P, J // 4], I32, name="picked_scales", align_bytes=64)
         moved_scales = keep.tile([P, J // 4], I32, name="moved_scales", align_bytes=64)
         picked_words = keep.tile([P, J], I32, name="picked_words", align_bytes=64)
-        v_codes = keep.tile([P, PASSES, 2 * J], U8, name="v_codes", align_bytes=64)
         wd4_codes = keep.tile([P, 2 * N // 4], I32, name="wd4_codes", align_bytes=64)
         wd8_codes = keep.tile([P, N], I32, name="wd8_codes", align_bytes=64)
         wd_scales = keep.tile([P, 2, N // 4], I32, name="wd_scales", align_bytes=64)
@@ -64,9 +66,10 @@ def tile_list_gmlpt_tanh_res_none_kernel(
         for name, w in (("g", wg), ("u", wu)):
             for a in range(PASSES):
                 raw[name, a] = keep.tile([P, PACK, R], F32, name="raw_%s%d" % (name, a))
-                nc.sync.dma_start(
-                    raw[name, a][:], w[a * K_PASS : (a + 1) * K_PASS, :].rearrange("(p j) c -> p j c", j=PACK)
-                )
+                rows = w[a * K_PASS : (a + 1) * K_PASS, :].rearrange("(p j) c -> p j c", j=PACK)
+                pieces = LAST_PIECES if (name, a) == ("u", PASSES - 1) else ((0, R),)
+                for c0, c1 in pieces:
+                    nc.sync.dma_start(raw[name, a][:, :, c0:c1], rows[:, :, c0:c1])
         nc.sync.dma_start(wd4_codes[:], wd4_words[0].bitcast(I32))
         nc.sync.dma_start(wd8_codes[:], wd8_words[0].rearrange("p n b -> p (n b)").bitcast(I32))
         for f, scales in enumerate((wd4_scales, wd8_scales)):
@@ -74,15 +77,17 @@ def tile_list_gmlpt_tanh_res_none_kernel(
             for r in range(4):
                 nc.sync.dma_start(wd_scales[r:P:32, f, :], rows[r])
 
-        grouped = [keep.tile([P, 2, P * PACK], BF16, name="grouped%d" % u, align_bytes=64) for u in range(2)]
-        w_codes, w_scales = {}, {}
+        grouped, w_codes, w_scales, v_codes = {}, {}, {}, {}
         for key in raw:
+            for u in range(2):
+                tag = "staging_%s%d%d" % (key[0], key[1], u)
+                grouped[key, u] = keep.tile([P, 2, P * PACK], BF16, name=tag, tag=tag, align_bytes=64)
             w_codes[key] = keep.tile([P, R], U32, name="w_codes_%s%d" % key, align_bytes=64)
             w_scales[key] = keep.tile([P, R], U8, name="w_scales_%s%d" % key, align_bytes=64)
 
-        def cast(key, u, copy):
-            src = raw[key][:].rearrange("p j (m u e) -> p u m j e", u=2, e=2)[:, u]
-            dst = grouped[u][:].rearrange("p e (m j) -> p m j e", j=PACK)
+        def cast(key, u, copy, c0=0, c1=R):
+            src = raw[key][:, :, c0:c1].rearrange("p j (m u e) -> p u m j e", u=2, e=2)[:, u]
+            dst = grouped[key, u][:, :, c0:c1].rearrange("p e (m j) -> p m j e", j=PACK)
             copy(dst, src)
 
         def quantize_weight(key, u):
@@ -90,7 +95,7 @@ def tile_list_gmlpt_tanh_res_none_kernel(
             nc.vector.quantize_mx(
                 out=w_codes[key][:, cols].bitcast(FP8X4),
                 scales=w_scales[key][:, cols],
-                in_=grouped[u][:].rearrange("p e x -> p (e x)"),
+                in_=grouped[key, u][:].rearrange("p e x -> p (e x)"),
             )
 
         def gather_words(h):
@@ -99,10 +104,10 @@ def tile_list_gmlpt_tanh_res_none_kernel(
                 word_window[:].bitcast(U32).indirect(offsets[:, h * HALF // 16 : (h + 1) * HALF // 16]),
             )
 
-        def part_words(h):
+        def part_words(h, tag):
+            v_codes[h] = keep.tile([P, PASSES, 2 * HALF], U8, name="v_codes%d" % h, tag=tag, align_bytes=64)
             src = picked_words[:, h * HALF : (h + 1) * HALF].bitcast(U16).rearrange("p (j d) -> p d j", d=2)
-            dst = v_codes[:, :, 2 * h * HALF : 2 * (h + 1) * HALF].bitcast(U16)
-            nc.vector.tensor_copy(dst, src)
+            nc.vector.tensor_copy(v_codes[h][:].bitcast(U16), src)
 
         v_scales = (picked_scales[:].bitcast(U8), moved_scales[:].bitcast(U8))
 
@@ -112,7 +117,7 @@ def tile_list_gmlpt_tanh_res_none_kernel(
                 out=acc,
                 lhsT=w_codes[key][:, t * P : (t + 1) * P].bitcast(FP8X4),
                 lhsT_scale=w_scales[key][:, t * P : (t + 1) * P],
-                rhs=v_codes[:, a, 2 * j0 : 2 * (j0 + width)].bitcast(FP4X4),
+                rhs=v_codes[j0 // HALF][:, a, 2 * (j0 % HALF) : 2 * (j0 % HALF + width)].bitcast(FP4X4),
                 rhs_scale=v_scales[a][:, j0 : j0 + width],
                 start=(a == 0),
                 stop=(a == PASSES - 1),
@@ -121,36 +126,38 @@ def tile_list_gmlpt_tanh_res_none_kernel(
         nc.vector.tensor_copy(picked_scales[:].bitcast(U8), scale_window[:].bitcast(U8).indirect(offsets[:]))
         nc.gpsimd.dma_start(moved_scales[0 : P - SHIFT, :], picked_scales[SHIFT:P, :])
         gather_words(0)
+        part_words(0, "v_codes0")
         gather_words(1)
-        part_words(0)
-        part_words(1)
         cast(("g", 0), 0, nc.scalar.copy)
         cast(("g", 0), 1, nc.scalar.copy)
         quantize_weight(("g", 0), 0)
-        cast(("g", 1), 0, nc.scalar.copy)
+        part_words(1, "staging_g00")
         quantize_weight(("g", 0), 1)
+        cast(("g", 1), 0, nc.scalar.copy)
         cast(("g", 1), 1, nc.scalar.copy)
         quantize_weight(("g", 1), 0)
-        cast(("u", 0), 0, nc.scalar.copy)
         quantize_weight(("g", 1), 1)
+        cast(("u", 0), 0, nc.scalar.copy)
         cast(("u", 0), 1, nc.vector.tensor_copy)
-        quantize_weight(("u", 0), 0)
-        cast(("u", 1), 0, nc.vector.tensor_copy)
         quantize_weight(("u", 0), 1)
-        cast(("u", 1), 1, nc.vector.tensor_copy)
+        quantize_weight(("u", 0), 0)
+        for c0, c1 in LAST_PIECES:
+            for u in range(2):
+                cast(("u", 1), u, nc.vector.tensor_copy, c0, c1)
         quantize_weight(("u", 1), 0)
         quantize_weight(("u", 1), 1)
 
-        gate_banks = {}
+        def new_bank(i):
+            return psum.tile([P, HALF], F32, name="bank%d" % i)
+
+        gate = (raw["u", 0], raw["g", 0])
         for h in range(2):
+            banks = [new_bank(i) for i in GATE_BANKS[h]]
+            for a in range(PASSES):
+                for t in range(PACK):
+                    first_layer_pass(banks[t][:], ("g", a), t, h * HALF, HALF)
             for t in range(PACK):
-                gate_banks[h, t] = psum.tile([P, HALF], F32, name="bank")
-                first_layer_pass(gate_banks[h, t][:], ("g", 0), t, h * HALF, HALF)
-        gate = keep.tile([P, PACK, J], F32, name="gate")
-        for h in range(2):
-            for t in range(PACK):
-                first_layer_pass(gate_banks[h, t][:], ("g", 1), t, h * HALF, HALF)
-                nc.scalar.activation(gate[:, t, h * HALF : (h + 1) * HALF], gate_banks[h, t][:], TANH)
+                nc.scalar.activation(gate[h][:, t, :], banks[t][:], TANH)
 
         hidden = keep.tile([P, J * PACK], BF16, name="hidden", align_bytes=64)
         h_codes = keep.tile([P, J], U32, name="h_codes", align_bytes=64)
@@ -161,14 +168,14 @@ def tile_list_gmlpt_tanh_res_none_kernel(
 
         def up_and_multiply(c):
             j0 = c * CHUNK
-            bank = psum.tile([P, HALF], F32, name="bank")
+            bank = new_bank(UP_BANKS[c % 4])
             for t in range(PACK):
                 for a in range(PASSES):
                     first_layer_pass(bank[:, t * CHUNK : (t + 1) * CHUNK], ("u", a), t, j0, CHUNK)
             nc.vector.tensor_tensor(
                 hidden[:, j0 * PACK : (j0 + CHUNK) * PACK].rearrange("p (c e t) -> p c t e", e=2, t=PACK),
                 bank[:].rearrange("p (t c e) -> p c t e", t=PACK, e=2),
-                gate[:, :, j0 : j0 + CHUNK].rearrange("p t (c e) -> p c t e", e=2),
+                gate[j0 // HALF][:, :, j0 % HALF : j0 % HALF + CHUNK].rearrange("p t (c e) -> p c t e", e=2),
                 MULT,
             )
 
@@ -198,22 +205,22 @@ def tile_list_gmlpt_tanh_res_none_kernel(
                 **moving
             )
 
-        def down_wide(j0):
-            for b in range(N // P):
-                bank = psum.tile([P, HALF], F32, name="bank")
-                down_group(bank[:], b, j0, HALF)
-                nc.scalar.copy(result[:, b, j0 : j0 + HALF], bank[:])
-                nc.sync.dma_start(out_rows[:, b, j0 : j0 + HALF], result[:, b, j0 : j0 + HALF])
+        def store(b0, b1, j0, width):
+            nc.sync.dma_start(out_rows[:, b0:b1, j0 : j0 + width], result[:, b0:b1, j0 : j0 + width])
 
-        def down_narrow(c):
+        def down_by_rows(j0, width, banks, copies):
+            for b in range(N // P):
+                bank = new_bank(banks[b])
+                down_group(bank[:, 0:width], b, j0, width)
+                copies[b](result[:, b, j0 : j0 + width], bank[:, 0:width])
+                store(b, b + 1, j0, width)
+
+        def down_chunk(c, i, copy):
             j0 = c * CHUNK
-            bank = psum.tile([P, HALF], F32, name="bank")
+            bank = new_bank(i)
             for b in range(N // P):
                 down_group(bank[:, b * CHUNK : (b + 1) * CHUNK], b, j0, CHUNK)
-            nc.scalar.copy(
-                result[:, :, j0 : j0 + CHUNK], bank[:, 0 : 2 * CHUNK].rearrange("p (b j) -> p b j", b=N // P)
-            )
-            nc.sync.dma_start(out_rows[:, :, j0 : j0 + CHUNK], result[:, :, j0 : j0 + CHUNK])
+            copy(result[:, :, j0 : j0 + CHUNK], bank[:, 0 : 2 * CHUNK].rearrange("p (b j) -> p b j", b=N // P))
 
         up_and_multiply(0)
         up_and_multiply(1)
@@ -223,14 +230,15 @@ def tile_list_gmlpt_tanh_res_none_kernel(
         up_and_multiply(4)
         quantize_hidden(2 * CHUNK, 2 * CHUNK)
         up_and_multiply(5)
-        quantize_hidden(4 * CHUNK, CHUNK)
         up_and_multiply(6)
-        quantize_hidden(5 * CHUNK, CHUNK)
+        quantize_hidden(4 * CHUNK, 2 * CHUNK)
         up_and_multiply(7)
         quantize_hidden(6 * CHUNK, CHUNK)
         quantize_hidden(7 * CHUNK, CHUNK)
-        down_wide(0)
-        down_narrow(4)
-        down_narrow(5)
-        down_narrow(6)
-        down_narrow(7)
+        down_by_rows(0, HALF, (4, 5), (nc.scalar.copy, nc.scalar.copy))
+        down_chunk(4, 0, nc.scalar.copy)
+        down_chunk(5, 1, nc.scalar.copy)
+        store(0, 2, 4 * CHUNK, 2 * CHUNK)
+        down_chunk(6, 6, nc.vector.tensor_copy)
+        store(0, 2, 6 * CHUNK, CHUNK)
+        down_by_rows(7 * CHUNK, CHUNK, (7, 2), (nc.scalar.copy, nc.vector.tensor_copy))

@@ -49,13 +49,13 @@ def tile_list_gmlpt_tanh_res_none_kernel(
         warm_out = keep.tile([P, 8], F32, name="warm_out")
 
         nc.gpsimd.memset(scale_window[:], 0)
-        nc.vector.memset(warm[:], 0.0)
-        nc.gpsimd.memset(moved_scales[:], 0)
         nc.gpsimd.memset(wd_scales[:], 0)
+        nc.vector.memset(warm[:], 0.0)
+        nc.vector.memset(moved_scales[:], 0)
 
-        nc.sync.dma_start(offsets[:], offs)
         table_words = tab_words[0].rearrange("p t b -> p (t b)").bitcast(I32)
         nc.sync.dma_start(word_window[:, 0 : T // 2], table_words[:, 0 : T // 2])
+        nc.sync.dma_start(offsets[:], offs)
         scale_rows = tab_scales.bitcast(I32).rearrange("a (q r) t -> r q a t", r=4)
         for r in range(4):
             nc.sync.dma_start(scale_window[r:P:SHIFT, :], scale_rows[r])
@@ -75,7 +75,7 @@ def tile_list_gmlpt_tanh_res_none_kernel(
         for f, scales in enumerate((wd4_scales, wd8_scales)):
             rows = scales[0].bitcast(I32).rearrange("(q r) n -> r q n", r=4)
             for r in range(4):
-                nc.sync.dma_start(wd_scales[r:P:32, f, :], rows[r])
+                nc.gpsimd.dma_start(wd_scales[r:P:32, f, :], rows[r])
 
         grouped, w_codes, w_scales, v_codes = {}, {}, {}, {}
         for key in raw:
@@ -124,7 +124,7 @@ def tile_list_gmlpt_tanh_res_none_kernel(
             )
 
         nc.vector.tensor_copy(picked_scales[:].bitcast(U8), scale_window[:].bitcast(U8).indirect(offsets[:]))
-        nc.gpsimd.dma_start(moved_scales[0 : P - SHIFT, :], picked_scales[SHIFT:P, :])
+        nc.scalar.dma_start(moved_scales[0 : P - SHIFT, :], picked_scales[SHIFT:P, :])
         gather_words(0)
         part_words(0, "v_codes0")
         gather_words(1)
@@ -231,11 +231,11 @@ def tile_list_gmlpt_tanh_res_none_kernel(
         quantize_hidden(2 * CHUNK, 2 * CHUNK)
         up_and_multiply(5)
         up_and_multiply(6)
+        down_by_rows(0, HALF, (4, 5), (nc.scalar.copy, nc.scalar.copy))
         quantize_hidden(4 * CHUNK, 2 * CHUNK)
         up_and_multiply(7)
         quantize_hidden(6 * CHUNK, CHUNK)
         quantize_hidden(7 * CHUNK, CHUNK)
-        down_by_rows(0, HALF, (4, 5), (nc.scalar.copy, nc.scalar.copy))
         down_chunk(4, 0, nc.scalar.copy)
         down_chunk(5, 1, nc.scalar.copy)
         store(0, 2, 4 * CHUNK, 2 * CHUNK)

@@ -23,8 +23,7 @@ PASSES = K // K_PASS
 HALF = 512
 CHUNK = 128
 SHIFT = 16
-GATE_BANKS = ((0, 1, 2, 3), (4, 5, 0, 1))
-UP_BANKS = (6, 7, 2, 3)
+FIRST_WORDS = 512
 LAST_PIECES = ((0, 384), (384, R))
 
 
@@ -48,28 +47,36 @@ def tile_list_gmlpt_tanh_res_none_kernel(
         warm = keep.tile([P, 8], F32, name="warm")
         warm_out = keep.tile([P, 8], F32, name="warm_out")
 
-        nc.gpsimd.memset(scale_window[:], 0)
+        nc.vector.memset(scale_window[:, 0 : T // 8], 0)
+        nc.gpsimd.memset(scale_window[:, T // 8 : T // 4], 0)
+        nc.gpsimd.memset(warm[:], 0.0)
         nc.gpsimd.memset(wd_scales[:], 0)
-        nc.vector.memset(warm[:], 0.0)
         nc.vector.memset(moved_scales[:], 0)
 
         table_words = tab_words[0].rearrange("p t b -> p (t b)").bitcast(I32)
-        nc.sync.dma_start(word_window[:, 0 : T // 2], table_words[:, 0 : T // 2])
+        nc.sync.dma_start(word_window[:, 0:FIRST_WORDS], table_words[:, 0:FIRST_WORDS])
         nc.sync.dma_start(offsets[:], offs)
         scale_rows = tab_scales.bitcast(I32).rearrange("a (q r) t -> r q a t", r=4)
         for r in range(4):
             nc.sync.dma_start(scale_window[r:P:SHIFT, :], scale_rows[r])
-        nc.sync.dma_start(word_window[:, T // 2 : T], table_words[:, T // 2 : T])
+        nc.sync.dma_start(word_window[:, FIRST_WORDS:T], table_words[:, FIRST_WORDS:T])
         nc.scalar.activation(warm_out[:], warm[:], TANH)
 
         raw = {}
-        for name, w in (("g", wg), ("u", wu)):
-            for a in range(PASSES):
-                raw[name, a] = keep.tile([P, PACK, R], F32, name="raw_%s%d" % (name, a))
-                rows = w[a * K_PASS : (a + 1) * K_PASS, :].rearrange("(p j) c -> p j c", j=PACK)
-                pieces = LAST_PIECES if (name, a) == ("u", PASSES - 1) else ((0, R),)
-                for c0, c1 in pieces:
-                    nc.sync.dma_start(raw[name, a][:, :, c0:c1], rows[:, :, c0:c1])
+
+        def load_weight(name, w, a, pieces):
+            raw[name, a] = keep.tile([P, PACK, R], F32, name="raw_%s%d" % (name, a))
+            rows = w[a * K_PASS : (a + 1) * K_PASS, :].rearrange("(p j) c -> p j c", j=PACK)
+            for c0, c1 in pieces:
+                nc.sync.dma_start(raw[name, a][:, :, c0:c1], rows[:, :, c0:c1])
+
+        load_weight("g", wg, 0, ((0, R),))
+        load_weight("g", wg, 1, ((0, R),))
+        nc.vector.tensor_copy(picked_scales[:].bitcast(U8), scale_window[:].bitcast(U8).indirect(offsets[:]))
+        for r in range(4):
+            nc.sync.dma_start(moved_scales[r:P:32, :], picked_scales[SHIFT + r : P : 32, :])
+        load_weight("u", wu, 0, ((0, R),))
+        load_weight("u", wu, 1, LAST_PIECES)
         nc.sync.dma_start(wd4_codes[:], wd4_words[0].bitcast(I32))
         nc.sync.dma_start(wd8_codes[:], wd8_words[0].rearrange("p n b -> p (n b)").bitcast(I32))
         for f, scales in enumerate((wd4_scales, wd8_scales)):
@@ -111,7 +118,7 @@ def tile_list_gmlpt_tanh_res_none_kernel(
 
         v_scales = (picked_scales[:].bitcast(U8), moved_scales[:].bitcast(U8))
 
-        def first_layer_pass(acc, key, t, j0, width):
+        def first_layer_pass(acc, key, t, j0, width, start, stop):
             a = key[1]
             nc.tensor.matmul_mx(
                 out=acc,
@@ -119,15 +126,13 @@ def tile_list_gmlpt_tanh_res_none_kernel(
                 lhsT_scale=w_scales[key][:, t * P : (t + 1) * P],
                 rhs=v_codes[j0 // HALF][:, a, 2 * (j0 % HALF) : 2 * (j0 % HALF + width)].bitcast(FP4X4),
                 rhs_scale=v_scales[a][:, j0 : j0 + width],
-                start=(a == 0),
-                stop=(a == PASSES - 1),
+                start=start,
+                stop=stop,
             )
 
-        nc.vector.tensor_copy(picked_scales[:].bitcast(U8), scale_window[:].bitcast(U8).indirect(offsets[:]))
-        nc.scalar.dma_start(moved_scales[0 : P - SHIFT, :], picked_scales[SHIFT:P, :])
         gather_words(0)
-        part_words(0, "v_codes0")
         gather_words(1)
+        part_words(0, "v_codes0")
         cast(("g", 0), 0, nc.scalar.copy)
         cast(("g", 0), 1, nc.scalar.copy)
         quantize_weight(("g", 0), 0)
@@ -151,13 +156,15 @@ def tile_list_gmlpt_tanh_res_none_kernel(
             return psum.tile([P, HALF], F32, name="bank%d" % i)
 
         gate = (raw["u", 0], raw["g", 0])
+        gate_banks = [new_bank(i) for i in range(2 * PACK)]
+        for u in range(2):
+            for h in range(2):
+                for t in (2 * u, 2 * u + 1):
+                    first_layer_pass(gate_banks[h * PACK + t][:], ("g", 0), t, h * HALF, HALF, True, False)
         for h in range(2):
-            banks = [new_bank(i) for i in GATE_BANKS[h]]
-            for a in range(PASSES):
-                for t in range(PACK):
-                    first_layer_pass(banks[t][:], ("g", a), t, h * HALF, HALF)
             for t in range(PACK):
-                nc.scalar.activation(gate[h][:, t, :], banks[t][:], TANH)
+                first_layer_pass(gate_banks[h * PACK + t][:], ("g", 1), t, h * HALF, HALF, False, True)
+                nc.scalar.activation(gate[h][:, t, :], gate_banks[h * PACK + t][:], TANH)
 
         hidden = keep.tile([P, J * PACK], BF16, name="hidden", align_bytes=64)
         h_codes = keep.tile([P, J], U32, name="h_codes", align_bytes=64)
@@ -166,12 +173,20 @@ def tile_list_gmlpt_tanh_res_none_kernel(
         out_rows = out.rearrange("(b p) j -> p b j", p=P)
         wd_planes = wd_scales[:].bitcast(U8)
 
+        up_banks = {}
+
+        def up_first(c):
+            up_banks[c] = new_bank(c)
+            for t in range(PACK):
+                first_layer_pass(up_banks[c][:, t * CHUNK : (t + 1) * CHUNK], ("u", 0), t, c * CHUNK, CHUNK, t == 0, False)
+
         def up_and_multiply(c):
             j0 = c * CHUNK
-            bank = new_bank(UP_BANKS[c % 4])
+            bank = up_banks[c]
             for t in range(PACK):
-                for a in range(PASSES):
-                    first_layer_pass(bank[:, t * CHUNK : (t + 1) * CHUNK], ("u", a), t, j0, CHUNK)
+                first_layer_pass(bank[:, t * CHUNK : (t + 1) * CHUNK], ("u", 1), t, j0, CHUNK, False, t == PACK - 1)
+            if c + 4 < J // CHUNK:
+                up_first(c + 4)
             nc.vector.tensor_tensor(
                 hidden[:, j0 * PACK : (j0 + CHUNK) * PACK].rearrange("p (c e t) -> p c t e", e=2, t=PACK),
                 bank[:].rearrange("p (t c e) -> p c t e", t=PACK, e=2),
@@ -222,6 +237,8 @@ def tile_list_gmlpt_tanh_res_none_kernel(
                 down_group(bank[:, b * CHUNK : (b + 1) * CHUNK], b, j0, CHUNK)
             copy(result[:, :, j0 : j0 + CHUNK], bank[:, 0 : 2 * CHUNK].rearrange("p (b j) -> p b j", b=N // P))
 
+        for c in range(4):
+            up_first(c)
         up_and_multiply(0)
         up_and_multiply(1)
         up_and_multiply(2)
@@ -231,14 +248,14 @@ def tile_list_gmlpt_tanh_res_none_kernel(
         quantize_hidden(2 * CHUNK, 2 * CHUNK)
         up_and_multiply(5)
         up_and_multiply(6)
-        down_by_rows(0, HALF, (4, 5), (nc.scalar.copy, nc.scalar.copy))
+        down_by_rows(0, HALF, (0, 1), (nc.scalar.copy, nc.scalar.copy))
         quantize_hidden(4 * CHUNK, 2 * CHUNK)
         up_and_multiply(7)
         quantize_hidden(6 * CHUNK, CHUNK)
         quantize_hidden(7 * CHUNK, CHUNK)
-        down_chunk(4, 0, nc.scalar.copy)
-        down_chunk(5, 1, nc.scalar.copy)
+        down_chunk(4, 2, nc.scalar.copy)
+        down_chunk(5, 3, nc.scalar.copy)
         store(0, 2, 4 * CHUNK, 2 * CHUNK)
-        down_chunk(6, 6, nc.vector.tensor_copy)
+        down_chunk(6, 4, nc.vector.tensor_copy)
         store(0, 2, 6 * CHUNK, CHUNK)
-        down_by_rows(7 * CHUNK, CHUNK, (7, 2), (nc.scalar.copy, nc.vector.tensor_copy))
+        down_by_rows(7 * CHUNK, CHUNK, (5, 6), (nc.scalar.copy, nc.vector.tensor_copy))

@@ -65,7 +65,7 @@ def tile_list_gmlpt_tanh_res_none_kernel(
         raw = {}
 
         def load_weight(name, w, a, pieces):
-            raw[name, a] = keep.tile([P, PACK, R], F32, name="raw_%s%d" % (name, a))
+            raw[name, a] = keep.tile([P, PACK, R], F32, name="raw_%s%d" % (name, a), tag="raw_%s%d" % (name, a))
             rows = w[a * K_PASS : (a + 1) * K_PASS, :].rearrange("(p j) c -> p j c", j=PACK)
             for c0, c1 in pieces:
                 nc.sync.dma_start(raw[name, a][:, :, c0:c1], rows[:, :, c0:c1])
@@ -155,7 +155,8 @@ def tile_list_gmlpt_tanh_res_none_kernel(
         def new_bank(i):
             return psum.tile([P, HALF], F32, name="bank%d" % i)
 
-        gate = (raw["u", 0], raw["g", 0])
+        gate_tile = keep.tile([P, 2, PACK, HALF], F32, name="gate", tag="raw_u0")
+        gate = (gate_tile[:, 0], gate_tile[:, 1])
         gate_banks = [new_bank(i) for i in range(2 * PACK)]
         for u in range(2):
             for h in range(2):
@@ -175,18 +176,16 @@ def tile_list_gmlpt_tanh_res_none_kernel(
 
         up_banks = {}
 
-        def up_first(c):
-            up_banks[c] = new_bank(c)
+        def up_passes(c, a, opens):
+            if opens:
+                up_banks[c] = new_bank(c)
             for t in range(PACK):
-                first_layer_pass(up_banks[c][:, t * CHUNK : (t + 1) * CHUNK], ("u", 0), t, c * CHUNK, CHUNK, t == 0, False)
+                acc = up_banks[c][:, t * CHUNK : (t + 1) * CHUNK]
+                first_layer_pass(acc, ("u", a), t, c * CHUNK, CHUNK, opens and t == 0, not opens and t == PACK - 1)
 
         def up_and_multiply(c):
             j0 = c * CHUNK
             bank = up_banks[c]
-            for t in range(PACK):
-                first_layer_pass(bank[:, t * CHUNK : (t + 1) * CHUNK], ("u", 1), t, j0, CHUNK, False, t == PACK - 1)
-            if c + 4 < J // CHUNK:
-                up_first(c + 4)
             nc.vector.tensor_tensor(
                 hidden[:, j0 * PACK : (j0 + CHUNK) * PACK].rearrange("p (c e t) -> p c t e", e=2, t=PACK),
                 bank[:].rearrange("p (t c e) -> p c t e", t=PACK, e=2),
@@ -238,7 +237,12 @@ def tile_list_gmlpt_tanh_res_none_kernel(
             copy(result[:, :, j0 : j0 + CHUNK], bank[:, 0 : 2 * CHUNK].rearrange("p (b j) -> p b j", b=N // P))
 
         for c in range(4):
-            up_first(c)
+            up_passes(c, 0, True)
+        for c in range(4):
+            up_passes(c, 1, False)
+        for c in range(4, 8):
+            up_passes(c, 1, True)
+            up_passes(c, 0, False)
         up_and_multiply(0)
         up_and_multiply(1)
         up_and_multiply(2)

@@ -24,6 +24,7 @@ HALF = 512
 CHUNK = 128
 SHIFT = 16
 FIRST_WORDS = 512
+EARLY = 3
 LAST_PIECES = ((0, 384), (384, R))
 
 
@@ -82,7 +83,7 @@ def tile_list_gmlpt_tanh_res_none_kernel(
         for f, scales in enumerate((wd4_scales, wd8_scales)):
             rows = scales[0].bitcast(I32).rearrange("(q r) n -> r q n", r=4)
             for r in range(4):
-                nc.gpsimd.dma_start(wd_scales[r:P:32, f, :], rows[r])
+                nc.sync.dma_start(wd_scales[r:P:32, f, :], rows[r])
 
         grouped, w_codes, w_scales, v_codes = {}, {}, {}, {}
         for key in raw:
@@ -236,11 +237,11 @@ def tile_list_gmlpt_tanh_res_none_kernel(
                 down_group(bank[:, b * CHUNK : (b + 1) * CHUNK], b, j0, CHUNK)
             copy(result[:, :, j0 : j0 + CHUNK], bank[:, 0 : 2 * CHUNK].rearrange("p (b j) -> p b j", b=N // P))
 
-        for c in range(4):
+        for c in range(EARLY):
             up_passes(c, 0, True)
-        for c in range(4):
+        for c in range(EARLY):
             up_passes(c, 1, False)
-        for c in range(4, 8):
+        for c in range(EARLY, 8):
             up_passes(c, 1, True)
             up_passes(c, 0, False)
         up_and_multiply(0)

@@ -24,7 +24,7 @@ HALF = 512
 CHUNK = 128
 SHIFT = 16
 FIRST_WORDS = 512
-EARLY = 3
+EARLY = 1
 LAST_PIECES = ((0, 384), (384, R))
 
 
@@ -77,7 +77,7 @@ def tile_list_gmlpt_tanh_res_none_kernel(
         for r in range(4):
             nc.sync.dma_start(moved_scales[r:P:32, :], picked_scales[SHIFT + r : P : 32, :])
         load_weight("u", wu, 0, ((0, R),))
-        load_weight("u", wu, 1, LAST_PIECES)
+        load_weight("u", wu, 1, ((0, R),))
         nc.sync.dma_start(wd4_codes[:], wd4_words[0].bitcast(I32))
         nc.sync.dma_start(wd8_codes[:], wd8_words[0].rearrange("p n b -> p (n b)").bitcast(I32))
         for f, scales in enumerate((wd4_scales, wd8_scales)):
@@ -87,9 +87,13 @@ def tile_list_gmlpt_tanh_res_none_kernel(
 
         grouped, w_codes, w_scales, v_codes = {}, {}, {}, {}
         for key in raw:
-            for u in range(2):
-                tag = "staging_%s%d%d" % (key[0], key[1], u)
-                grouped[key, u] = keep.tile([P, 2, P * PACK], BF16, name=tag, tag=tag, align_bytes=64)
+            if key == ("g", 1):
+                whole = keep.tile([P, PACK, P * PACK], BF16, name="staging_g1", align_bytes=64)
+                grouped[key, 0], grouped[key, 1] = whole[:, 0:2], whole[:, 2:4]
+            else:
+                for u in range(2):
+                    tag = "staging_%s%d%d" % (key[0], key[1], u)
+                    grouped[key, u] = keep.tile([P, 2, P * PACK], BF16, name=tag, tag=tag, align_bytes=64)
             w_codes[key] = keep.tile([P, R], U32, name="w_codes_%s%d" % key, align_bytes=64)
             w_scales[key] = keep.tile([P, R], U8, name="w_scales_%s%d" % key, align_bytes=64)
 
@@ -141,32 +145,53 @@ def tile_list_gmlpt_tanh_res_none_kernel(
         quantize_weight(("g", 0), 1)
         cast(("g", 1), 0, nc.scalar.copy)
         cast(("g", 1), 1, nc.scalar.copy)
-        quantize_weight(("g", 1), 0)
-        quantize_weight(("g", 1), 1)
+        nc.vector.quantize_mx(
+            out=w_codes["g", 1][:].bitcast(FP8X4),
+            scales=w_scales["g", 1][:],
+            in_=whole[:].rearrange("p t x -> p (t x)"),
+        )
         cast(("u", 0), 0, nc.scalar.copy)
         cast(("u", 0), 1, nc.vector.tensor_copy)
         quantize_weight(("u", 0), 1)
         quantize_weight(("u", 0), 0)
-        for c0, c1 in LAST_PIECES:
-            for u in range(2):
-                cast(("u", 1), u, nc.vector.tensor_copy, c0, c1)
+        cast(("u", 1), 0, nc.vector.tensor_copy)
+        cast(("u", 1), 1, nc.scalar.copy)
         quantize_weight(("u", 1), 0)
         quantize_weight(("u", 1), 1)
 
         def new_bank(i):
             return psum.tile([P, HALF], F32, name="bank%d" % i)
 
-        gate_tile = keep.tile([P, 2, PACK, HALF], F32, name="gate", tag="raw_u0")
-        gate = (gate_tile[:, 0], gate_tile[:, 1])
+        gate_first = keep.tile([P, CHUNK * PACK], F32, name="gate_first", tag="raw_u0")
+        gate_rest = keep.tile([P, 7 * CHUNK * PACK], F32, name="gate_rest", tag="raw_u1")
+        gate_chunks = ((gate_first, 0), (gate_rest, 0), (gate_rest, 1), (gate_rest, 2))
+        gate_rows = gate_rest[:, 3 * CHUNK * PACK :].rearrange("p (t j) -> p t j", t=PACK)
         gate_banks = [new_bank(i) for i in range(2 * PACK)]
+
+        def token_major(bank):
+            return bank[:].rearrange("p (t j) -> p j t", t=PACK)
+
+        def chunk_of(tile, c):
+            return tile[:, c * CHUNK * PACK : (c + 1) * CHUNK * PACK].rearrange("p (j t) -> p j t", t=PACK)
+
+        def gate_chunk(c, a, tiles):
+            for t in tiles:
+                acc = gate_banks[c][:, t * CHUNK : (t + 1) * CHUNK]
+                first_layer_pass(acc, ("g", a), t, c * CHUNK, CHUNK, a == 0 and t == 0, a == 1 and t == PACK - 1)
+
         for u in range(2):
-            for h in range(2):
-                for t in (2 * u, 2 * u + 1):
-                    first_layer_pass(gate_banks[h * PACK + t][:], ("g", 0), t, h * HALF, HALF, True, False)
-        for h in range(2):
-            for t in range(PACK):
-                first_layer_pass(gate_banks[h * PACK + t][:], ("g", 1), t, h * HALF, HALF, False, True)
-                nc.scalar.activation(gate[h][:, t, :], gate_banks[h * PACK + t][:], TANH)
+            for c in range(4):
+                gate_chunk(c, 0, (2 * u, 2 * u + 1))
+            for t in (2 * u, 2 * u + 1):
+                first_layer_pass(gate_banks[PACK + t][:], ("g", 0), t, HALF, HALF, True, False)
+        for c in range(4):
+            gate_chunk(c, 1, range(PACK))
+        for t in range(PACK):
+            first_layer_pass(gate_banks[PACK + t][:], ("g", 1), t, HALF, HALF, False, True)
+        for c in range(4):
+            nc.scalar.activation(chunk_of(*gate_chunks[c]), token_major(gate_banks[c]), TANH)
+        for t in range(PACK):
+            nc.scalar.activation(gate_rows[:, t, :], gate_banks[PACK + t][:], TANH)
 
         hidden = keep.tile([P, J * PACK], BF16, name="hidden", align_bytes=64)
         h_codes = keep.tile([P, J], U32, name="h_codes", align_bytes=64)
@@ -187,10 +212,13 @@ def tile_list_gmlpt_tanh_res_none_kernel(
         def up_and_multiply(c):
             j0 = c * CHUNK
             bank = up_banks[c]
+            if c < 4:
+                nc.vector.tensor_tensor(chunk_of(hidden, c), token_major(bank), chunk_of(*gate_chunks[c]), MULT)
+                return
             nc.vector.tensor_tensor(
                 hidden[:, j0 * PACK : (j0 + CHUNK) * PACK].rearrange("p (c e t) -> p c t e", e=2, t=PACK),
                 bank[:].rearrange("p (t c e) -> p c t e", t=PACK, e=2),
-                gate[j0 // HALF][:, :, j0 % HALF : j0 % HALF + CHUNK].rearrange("p t (c e) -> p c t e", e=2),
+                gate_rows[:, :, j0 % HALF : j0 % HALF + CHUNK].rearrange("p t (c e) -> p c t e", e=2),
                 MULT,
             )
 

@@ -23,7 +23,7 @@ PASSES = K // K_PASS
 HALF = 512
 CHUNK = 128
 SHIFT = 16
-FIRST_WORDS = 512
+FIRST_WORDS = 704
 EARLY = 1
 LAST_PIECES = ((0, 384), (384, R))
 
@@ -48,11 +48,10 @@ def tile_list_gmlpt_tanh_res_none_kernel(
         warm = keep.tile([P, 8], F32, name="warm")
         warm_out = keep.tile([P, 8], F32, name="warm_out")
 
-        nc.vector.memset(scale_window[:, 0 : T // 8], 0)
-        nc.gpsimd.memset(scale_window[:, T // 8 : T // 4], 0)
-        nc.gpsimd.memset(warm[:], 0.0)
-        nc.gpsimd.memset(wd_scales[:], 0)
+        nc.vector.memset(scale_window[:], 0)
+        nc.vector.memset(warm[:], 0.0)
         nc.vector.memset(moved_scales[:], 0)
+        nc.vector.memset(wd_scales[:], 0)
 
         table_words = tab_words[0].rearrange("p t b -> p (t b)").bitcast(I32)
         nc.sync.dma_start(word_window[:, 0:FIRST_WORDS], table_words[:, 0:FIRST_WORDS])
@@ -85,11 +84,11 @@ def tile_list_gmlpt_tanh_res_none_kernel(
             for r in range(4):
                 nc.sync.dma_start(wd_scales[r:P:32, f, :], rows[r])
 
-        grouped, w_codes, w_scales, v_codes = {}, {}, {}, {}
+        grouped, whole, w_codes, w_scales, v_codes = {}, {}, {}, {}, {}
         for key in raw:
-            if key == ("g", 1):
-                whole = keep.tile([P, PACK, P * PACK], BF16, name="staging_g1", align_bytes=64)
-                grouped[key, 0], grouped[key, 1] = whole[:, 0:2], whole[:, 2:4]
+            if key in (("g", 1), ("u", 0)):
+                whole[key] = keep.tile([P, PACK, P * PACK], BF16, name="staging_%s%d" % key, align_bytes=64)
+                grouped[key, 0], grouped[key, 1] = whole[key][:, 0:2], whole[key][:, 2:4]
             else:
                 for u in range(2):
                     tag = "staging_%s%d%d" % (key[0], key[1], u)
@@ -108,6 +107,13 @@ def tile_list_gmlpt_tanh_res_none_kernel(
                 out=w_codes[key][:, cols].bitcast(FP8X4),
                 scales=w_scales[key][:, cols],
                 in_=grouped[key, u][:].rearrange("p e x -> p (e x)"),
+            )
+
+        def quantize_whole(key):
+            nc.vector.quantize_mx(
+                out=w_codes[key][:].bitcast(FP8X4),
+                scales=w_scales[key][:],
+                in_=whole[key][:].rearrange("p t x -> p (t x)"),
             )
 
         def gather_words(h):
@@ -145,15 +151,10 @@ def tile_list_gmlpt_tanh_res_none_kernel(
         quantize_weight(("g", 0), 1)
         cast(("g", 1), 0, nc.scalar.copy)
         cast(("g", 1), 1, nc.scalar.copy)
-        nc.vector.quantize_mx(
-            out=w_codes["g", 1][:].bitcast(FP8X4),
-            scales=w_scales["g", 1][:],
-            in_=whole[:].rearrange("p t x -> p (t x)"),
-        )
+        quantize_whole(("g", 1))
         cast(("u", 0), 0, nc.scalar.copy)
         cast(("u", 0), 1, nc.vector.tensor_copy)
-        quantize_weight(("u", 0), 1)
-        quantize_weight(("u", 0), 0)
+        quantize_whole(("u", 0))
         cast(("u", 1), 0, nc.vector.tensor_copy)
         cast(("u", 1), 1, nc.scalar.copy)
         quantize_weight(("u", 1), 0)

@@ -22,7 +22,6 @@ K_PASS = P * PACK
 PASSES = K // K_PASS
 HALF = 512
 CHUNK = 128
-SHIFT = 16
 FIRST_WORDS = 704
 EARLY = 1
 LAST_PIECES = ((0, 384), (384, R))
@@ -56,9 +55,10 @@ def tile_list_gmlpt_tanh_res_none_kernel(
         table_words = tab_words[0].rearrange("p t b -> p (t b)").bitcast(I32)
         nc.sync.dma_start(word_window[:, 0:FIRST_WORDS], table_words[:, 0:FIRST_WORDS])
         nc.sync.dma_start(offsets[:], offs)
-        scale_rows = tab_scales.bitcast(I32).rearrange("a (q r) t -> r q a t", r=4)
+        scale_rows = tab_scales.bitcast(I32)
         for r in range(4):
-            nc.sync.dma_start(scale_window[r:P:SHIFT, :], scale_rows[r])
+            nc.sync.dma_start(scale_window[r:P:32, :], scale_rows[0].rearrange("(q r) t -> r q t", r=4)[r])
+        nc.sync.dma_start(scale_window[4:P:8, :], scale_rows[1])
         nc.sync.dma_start(word_window[:, FIRST_WORDS:T], table_words[:, FIRST_WORDS:T])
         nc.scalar.activation(warm_out[:], warm[:], TANH)
 
@@ -74,7 +74,7 @@ def tile_list_gmlpt_tanh_res_none_kernel(
         load_weight("g", wg, 1, ((0, R),))
         nc.vector.tensor_copy(picked_scales[:].bitcast(U8), scale_window[:].bitcast(U8).indirect(offsets[:]))
         for r in range(4):
-            nc.sync.dma_start(moved_scales[r:P:32, :], picked_scales[SHIFT + r : P : 32, :])
+            nc.sync.dma_start(moved_scales[r:P:32, :], picked_scales[8 * r + 4 : P : 32, :])
         load_weight("u", wu, 0, ((0, R),))
         load_weight("u", wu, 1, ((0, R),))
         nc.sync.dma_start(wd4_codes[:], wd4_words[0].bitcast(I32))
@@ -190,9 +190,9 @@ def tile_list_gmlpt_tanh_res_none_kernel(
         for t in range(PACK):
             first_layer_pass(gate_banks[PACK + t][:], ("g", 1), t, HALF, HALF, False, True)
         for c in range(4):
-            nc.scalar.activation(chunk_of(*gate_chunks[c]), token_major(gate_banks[c]), TANH)
+            nc.scalar.activation(chunk_of(*gate_chunks[c]), token_major(gate_banks[c]), TANH, bias=warm_out[:, 0:1])
         for t in range(PACK):
-            nc.scalar.activation(gate_rows[:, t, :], gate_banks[PACK + t][:], TANH)
+            nc.scalar.activation(gate_rows[:, t, :], gate_banks[PACK + t][:], TANH, bias=warm_out[:, 0:1])
 
         hidden = keep.tile([P, J * PACK], BF16, name="hidden", align_bytes=64)
         h_codes = keep.tile([P, J], U32, name="h_codes", align_bytes=64)

@@ -22,9 +22,9 @@ K_PASS = P * PACK
 PASSES = K // K_PASS
 HALF = 512
 CHUNK = 128
-FIRST_WORDS = 704
-EARLY = 1
-LAST_PIECES = ((0, 384), (384, R))
+ROW0 = 96
+EARLY = 2
+SHARE = 256
 
 
 def tile_list_gmlpt_tanh_res_none_kernel(
@@ -39,7 +39,7 @@ def tile_list_gmlpt_tanh_res_none_kernel(
         scale_window = keep.tile([P, T // 4], I32, name="scale_window", align_bytes=64)
         word_window = keep.tile([P, T], I32, name="word_window", align_bytes=64)
         picked_scales = keep.tile([P, J // 4], I32, name="picked_scales", align_bytes=64)
-        moved_scales = keep.tile([P, J // 4], I32, name="moved_scales", align_bytes=64)
+        moved_scales = [keep.tile([P, J // 4], I32, name="moved_scales%d" % a, align_bytes=64) for a in range(PASSES)]
         picked_words = keep.tile([P, J], I32, name="picked_words", align_bytes=64)
         wd4_codes = keep.tile([P, 2 * N // 4], I32, name="wd4_codes", align_bytes=64)
         wd8_codes = keep.tile([P, N], I32, name="wd8_codes", align_bytes=64)
@@ -47,19 +47,15 @@ def tile_list_gmlpt_tanh_res_none_kernel(
         warm = keep.tile([P, 8], F32, name="warm")
         warm_out = keep.tile([P, 8], F32, name="warm_out")
 
-        nc.vector.memset(scale_window[:], 0)
+        nc.vector.memset(scale_window[0:ROW0, :], 0)
         nc.vector.memset(warm[:], 0.0)
-        nc.vector.memset(moved_scales[:], 0)
+        nc.vector.memset(moved_scales[0][:], 0)
+        nc.vector.memset(moved_scales[1][:], 0)
         nc.vector.memset(wd_scales[:], 0)
 
-        table_words = tab_words[0].rearrange("p t b -> p (t b)").bitcast(I32)
-        nc.sync.dma_start(word_window[:, 0:FIRST_WORDS], table_words[:, 0:FIRST_WORDS])
+        nc.sync.dma_start(scale_window[ROW0:P, :], tab_scales.bitcast(I32).rearrange("a q t -> (a q) t"))
         nc.sync.dma_start(offsets[:], offs)
-        scale_rows = tab_scales.bitcast(I32)
-        for r in range(4):
-            nc.sync.dma_start(scale_window[r:P:32, :], scale_rows[0].rearrange("(q r) t -> r q t", r=4)[r])
-        nc.sync.dma_start(scale_window[4:P:8, :], scale_rows[1])
-        nc.sync.dma_start(word_window[:, FIRST_WORDS:T], table_words[:, FIRST_WORDS:T])
+        nc.sync.dma_start(word_window[:], tab_words[0].rearrange("p t b -> p (t b)").bitcast(I32))
         nc.scalar.activation(warm_out[:], warm[:], TANH)
 
         raw = {}
@@ -70,11 +66,16 @@ def tile_list_gmlpt_tanh_res_none_kernel(
             for c0, c1 in pieces:
                 nc.sync.dma_start(raw[name, a][:, :, c0:c1], rows[:, :, c0:c1])
 
+        def move_scales(a):
+            for q in range(4):
+                first = ROW0 + 16 * a + 4 * q
+                nc.sync.dma_start(moved_scales[a][32 * q : 32 * q + 4, :], picked_scales[first : first + 4, :])
+
         load_weight("g", wg, 0, ((0, R),))
-        load_weight("g", wg, 1, ((0, R),))
         nc.vector.tensor_copy(picked_scales[:].bitcast(U8), scale_window[:].bitcast(U8).indirect(offsets[:]))
-        for r in range(4):
-            nc.sync.dma_start(moved_scales[r:P:32, :], picked_scales[8 * r + 4 : P : 32, :])
+        move_scales(0)
+        load_weight("g", wg, 1, ((0, R),))
+        move_scales(1)
         load_weight("u", wu, 0, ((0, R),))
         load_weight("u", wu, 1, ((0, R),))
         nc.sync.dma_start(wd4_codes[:], wd4_words[0].bitcast(I32))
@@ -127,7 +128,7 @@ def tile_list_gmlpt_tanh_res_none_kernel(
             src = picked_words[:, h * HALF : (h + 1) * HALF].bitcast(U16).rearrange("p (j d) -> p d j", d=2)
             nc.vector.tensor_copy(v_codes[h][:].bitcast(U16), src)
 
-        v_scales = (picked_scales[:].bitcast(U8), moved_scales[:].bitcast(U8))
+        v_scales = (moved_scales[0][:].bitcast(U8), moved_scales[1][:].bitcast(U8))
 
         def first_layer_pass(acc, key, t, j0, width, start, stop):
             a = key[1]
@@ -150,23 +151,24 @@ def tile_list_gmlpt_tanh_res_none_kernel(
         part_words(1, "staging_g00")
         quantize_weight(("g", 0), 1)
         cast(("g", 1), 0, nc.scalar.copy)
-        cast(("g", 1), 1, nc.scalar.copy)
+        cast(("g", 1), 1, nc.vector.tensor_copy)
         quantize_whole(("g", 1))
-        cast(("u", 0), 0, nc.scalar.copy)
+        cast(("u", 0), 0, nc.vector.tensor_copy)
         cast(("u", 0), 1, nc.vector.tensor_copy)
         quantize_whole(("u", 0))
         cast(("u", 1), 0, nc.vector.tensor_copy)
-        cast(("u", 1), 1, nc.scalar.copy)
+        cast(("u", 1), 1, nc.vector.tensor_copy, 0, SHARE)
+        cast(("u", 1), 1, nc.scalar.copy, SHARE, R)
         quantize_weight(("u", 1), 0)
         quantize_weight(("u", 1), 1)
 
         def new_bank(i):
             return psum.tile([P, HALF], F32, name="bank%d" % i)
 
-        gate_first = keep.tile([P, CHUNK * PACK], F32, name="gate_first", tag="raw_u0")
-        gate_rest = keep.tile([P, 7 * CHUNK * PACK], F32, name="gate_rest", tag="raw_u1")
-        gate_chunks = ((gate_first, 0), (gate_rest, 0), (gate_rest, 1), (gate_rest, 2))
-        gate_rows = gate_rest[:, 3 * CHUNK * PACK :].rearrange("p (t j) -> p t j", t=PACK)
+        gate_first = keep.tile([P, 2 * CHUNK * PACK], F32, name="gate_first")
+        gate_rest = keep.tile([P, 6 * CHUNK * PACK], F32, name="gate_rest", tag="raw_u1")
+        gate_chunks = ((gate_first, 0), (gate_first, 1), (gate_rest, 0), (gate_rest, 1))
+        gate_rows = gate_rest[:, 2 * CHUNK * PACK :].rearrange("p (t j) -> p t j", t=PACK)
         gate_banks = [new_bank(i) for i in range(2 * PACK)]
 
         def token_major(bank):
@@ -290,6 +292,6 @@ def tile_list_gmlpt_tanh_res_none_kernel(
         down_chunk(4, 2, nc.scalar.copy)
         down_chunk(5, 3, nc.scalar.copy)
         store(0, 2, 4 * CHUNK, 2 * CHUNK)
-        down_chunk(6, 4, nc.vector.tensor_copy)
+        down_chunk(6, 4, nc.scalar.copy)
         store(0, 2, 6 * CHUNK, CHUNK)
         down_by_rows(7 * CHUNK, CHUNK, (5, 6), (nc.scalar.copy, nc.vector.tensor_copy))

@@ -23,8 +23,9 @@ PASSES = K // K_PASS
 HALF = 512
 CHUNK = 128
 ROW0 = 96
-EARLY = 2
-SHARE = 256
+EARLY = 3
+SHARE = 128
+UP_BANKS = (0, 1, 2, 3, 4, 5, 3, 4)
 
 
 def tile_list_gmlpt_tanh_res_none_kernel(
@@ -80,10 +81,11 @@ def tile_list_gmlpt_tanh_res_none_kernel(
         load_weight("u", wu, 1, ((0, R),))
         nc.sync.dma_start(wd4_codes[:], wd4_words[0].bitcast(I32))
         nc.sync.dma_start(wd8_codes[:], wd8_words[0].rearrange("p n b -> p (n b)").bitcast(I32))
+
         for f, scales in enumerate((wd4_scales, wd8_scales)):
             rows = scales[0].bitcast(I32).rearrange("(q r) n -> r q n", r=4)
             for r in range(4):
-                nc.sync.dma_start(wd_scales[r:P:32, f, :], rows[r])
+                (nc.sync, nc.gpsimd)[f].dma_start(wd_scales[r:P:32, f, :], rows[r])
 
         grouped, whole, w_codes, w_scales, v_codes = {}, {}, {}, {}, {}
         for key in raw:
@@ -165,10 +167,10 @@ def tile_list_gmlpt_tanh_res_none_kernel(
         def new_bank(i):
             return psum.tile([P, HALF], F32, name="bank%d" % i)
 
-        gate_first = keep.tile([P, 2 * CHUNK * PACK], F32, name="gate_first")
-        gate_rest = keep.tile([P, 6 * CHUNK * PACK], F32, name="gate_rest", tag="raw_u1")
-        gate_chunks = ((gate_first, 0), (gate_first, 1), (gate_rest, 0), (gate_rest, 1))
-        gate_rows = gate_rest[:, 2 * CHUNK * PACK :].rearrange("p (t j) -> p t j", t=PACK)
+        gate_first = keep.tile([P, 3 * CHUNK * PACK], F32, name="gate_first")
+        gate_rest = keep.tile([P, 5 * CHUNK * PACK], F32, name="gate_rest", tag="raw_u1")
+        gate_chunks = ((gate_first, 0), (gate_first, 1), (gate_first, 2), (gate_rest, 0))
+        gate_rows = gate_rest[:, CHUNK * PACK :].rearrange("p (t j) -> p t j", t=PACK)
         gate_banks = [new_bank(i) for i in range(2 * PACK)]
 
         def token_major(bank):
@@ -207,7 +209,7 @@ def tile_list_gmlpt_tanh_res_none_kernel(
 
         def up_passes(c, a, opens):
             if opens:
-                up_banks[c] = new_bank(c)
+                up_banks[c] = new_bank(UP_BANKS[c])
             for t in range(PACK):
                 acc = up_banks[c][:, t * CHUNK : (t + 1) * CHUNK]
                 first_layer_pass(acc, ("u", a), t, c * CHUNK, CHUNK, opens and t == 0, not opens and t == PACK - 1)
@@ -268,30 +270,66 @@ def tile_list_gmlpt_tanh_res_none_kernel(
                 down_group(bank[:, b * CHUNK : (b + 1) * CHUNK], b, j0, CHUNK)
             copy(result[:, :, j0 : j0 + CHUNK], bank[:, 0 : 2 * CHUNK].rearrange("p (b j) -> p b j", b=N // P))
 
+        def down_pair(c, i):
+            j0 = c * CHUNK
+            bank = new_bank(i)
+            for b in range(N // P):
+                for e in range(2):
+                    cols = slice(j0 + e * CHUNK, j0 + (e + 1) * CHUNK)
+                    nc.tensor.matmul_mx(
+                        out=bank[:, (2 * b + e) * CHUNK : (2 * b + e + 1) * CHUNK],
+                        lhsT=wd4_codes[:].bitcast(U8)[:, 2 * b * P : 2 * (b + 1) * P].bitcast(FP4X4),
+                        lhsT_scale=wd_planes[:, 0, b * P : (b + 1) * P],
+                        rhs=h_codes[:, cols].bitcast(FP8X4),
+                        rhs_scale=h_scales[:, cols],
+                        start=e == 0,
+                        stop=False,
+                    )
+                cols = slice(j0, j0 + 2 * CHUNK)
+                nc.tensor.matmul_mx(
+                    out=bank[:, 2 * b * CHUNK : 2 * (b + 1) * CHUNK],
+                    lhsT=wd8_codes[:, b * P : (b + 1) * P].bitcast(FP8X4),
+                    lhsT_scale=wd_planes[:, 1, b * P : (b + 1) * P],
+                    rhs=h_codes[:, cols].bitcast(FP8X4),
+                    rhs_scale=h_scales[:, cols],
+                    start=False,
+                    stop=True,
+                )
+            nc.scalar.copy(result[:, :, j0 : j0 + 2 * CHUNK], bank[:].rearrange("p (b j) -> p b j", b=N // P))
+            store(0, 2, j0, 2 * CHUNK)
+
+        def up_both(c):
+            up_passes(c, 1, True)
+            up_passes(c, 0, False)
+
         for c in range(EARLY):
             up_passes(c, 0, True)
         for c in range(EARLY):
             up_passes(c, 1, False)
-        for c in range(EARLY, 8):
-            up_passes(c, 1, True)
-            up_passes(c, 0, False)
+        up_both(3)
+        up_both(4)
+        up_both(5)
         up_and_multiply(0)
         up_and_multiply(1)
         up_and_multiply(2)
         quantize_hidden(0, 2 * CHUNK)
+        down_pair(0, 0)
         up_and_multiply(3)
+        up_both(6)
         up_and_multiply(4)
+        up_both(7)
         quantize_hidden(2 * CHUNK, 2 * CHUNK)
+        down_pair(2, 1)
         up_and_multiply(5)
+        quantize_hidden(4 * CHUNK, CHUNK)
+        down_chunk(4, 2, nc.scalar.copy)
         up_and_multiply(6)
-        down_by_rows(0, HALF, (0, 1), (nc.scalar.copy, nc.scalar.copy))
-        quantize_hidden(4 * CHUNK, 2 * CHUNK)
+        quantize_hidden(5 * CHUNK, CHUNK)
+        down_chunk(5, 6, nc.scalar.copy)
+        store(0, 2, 4 * CHUNK, 2 * CHUNK)
         up_and_multiply(7)
         quantize_hidden(6 * CHUNK, CHUNK)
         quantize_hidden(7 * CHUNK, CHUNK)
-        down_chunk(4, 2, nc.scalar.copy)
-        down_chunk(5, 3, nc.scalar.copy)
-        store(0, 2, 4 * CHUNK, 2 * CHUNK)
-        down_chunk(6, 4, nc.scalar.copy)
+        down_chunk(6, 7, nc.scalar.copy)
         store(0, 2, 6 * CHUNK, CHUNK)
-        down_by_rows(7 * CHUNK, CHUNK, (5, 6), (nc.scalar.copy, nc.vector.tensor_copy))
+        down_by_rows(7 * CHUNK, CHUNK, (5, 0), (nc.scalar.copy, nc.vector.tensor_copy))

@@ -48,17 +48,23 @@ def tile_list_gmlpt_tanh_res_none_kernel(
         warm = keep.tile([P, 8], F32, name="warm")
         warm_out = keep.tile([P, 8], F32, name="warm_out")
 
+        nc.vector.memset(wd_scales[:], 0)
         nc.vector.memset(scale_window[0:ROW0, :], 0)
         nc.vector.memset(warm[:], 0.0)
         nc.vector.memset(moved_scales[0][:], 0)
         nc.vector.memset(moved_scales[1][:], 0)
-        nc.vector.memset(wd_scales[:], 0)
 
         nc.sync.dma_start(scale_window[ROW0:P, :], tab_scales.bitcast(I32).rearrange("a q t -> (a q) t"))
         nc.sync.dma_start(offsets[:], offs)
         nc.sync.dma_start(word_window[:], tab_words[0].rearrange("p t b -> p (t b)").bitcast(I32))
         nc.scalar.activation(warm_out[:], warm[:], TANH)
 
+        def load_down_scales(f, scales):
+            rows = scales[0].bitcast(I32).rearrange("(q r) n -> r q n", r=4)
+            for r in range(4):
+                nc.sync.dma_start(wd_scales[r:P:32, f, :], rows[r])
+
+        load_down_scales(0, wd4_scales)
         raw = {}
 
         def load_weight(name, w, a, pieces):
@@ -82,10 +88,7 @@ def tile_list_gmlpt_tanh_res_none_kernel(
         nc.sync.dma_start(wd4_codes[:], wd4_words[0].bitcast(I32))
         nc.sync.dma_start(wd8_codes[:], wd8_words[0].rearrange("p n b -> p (n b)").bitcast(I32))
 
-        for f, scales in enumerate((wd4_scales, wd8_scales)):
-            rows = scales[0].bitcast(I32).rearrange("(q r) n -> r q n", r=4)
-            for r in range(4):
-                (nc.sync, nc.gpsimd)[f].dma_start(wd_scales[r:P:32, f, :], rows[r])
+        load_down_scales(1, wd8_scales)
 
         grouped, whole, w_codes, w_scales, v_codes = {}, {}, {}, {}, {}
         for key in raw:

@@ -23,9 +23,11 @@ PASSES = K // K_PASS
 HALF = 512
 CHUNK = 128
 ROW0 = 96
-EARLY = 3
-SHARE = 128
-UP_BANKS = (0, 1, 2, 3, 4, 5, 3, 4)
+CHUNKS = J // CHUNK
+WARM_PASSES = 4
+EARLY = 4
+SHARE = 256
+UP_BANKS = (0, 1, 2, 3, 4, 5, 6, 7)
 
 
 def tile_list_gmlpt_tanh_res_none_kernel(
@@ -53,6 +55,11 @@ def tile_list_gmlpt_tanh_res_none_kernel(
         nc.vector.memset(warm[:], 0.0)
         nc.vector.memset(moved_scales[0][:], 0)
         nc.vector.memset(moved_scales[1][:], 0)
+        zeros = keep.tile([P, K_PASS], BF16, name="zeros", align_bytes=64)
+        zero_codes = keep.tile([P, P], U32, name="zero_codes", align_bytes=64)
+        zero_scales = keep.tile([P, P], U8, name="zero_scales", align_bytes=64)
+        nc.vector.memset(zeros[:], 0.0)
+        nc.vector.quantize_mx(out=zero_codes[:].bitcast(FP8X4), scales=zero_scales[:], in_=zeros[:])
 
         nc.sync.dma_start(scale_window[ROW0:P, :], tab_scales.bitcast(I32).rearrange("a q t -> (a q) t"))
         nc.sync.dma_start(offsets[:], offs)
@@ -92,7 +99,7 @@ def tile_list_gmlpt_tanh_res_none_kernel(
 
         grouped, whole, w_codes, w_scales, v_codes = {}, {}, {}, {}, {}
         for key in raw:
-            if key in (("g", 1), ("u", 0)):
+            if key == ("u", 0):
                 whole[key] = keep.tile([P, PACK, P * PACK], BF16, name="staging_%s%d" % key, align_bytes=64)
                 grouped[key, 0], grouped[key, 1] = whole[key][:, 0:2], whole[key][:, 2:4]
             else:
@@ -148,6 +155,17 @@ def tile_list_gmlpt_tanh_res_none_kernel(
             )
 
         gather_words(0)
+        idle_bank = psum.tile([P, HALF], F32, name="bank7")
+        for i in range(WARM_PASSES):
+            nc.tensor.matmul_mx(
+                out=idle_bank[:],
+                lhsT=zero_codes[:].bitcast(FP8X4),
+                lhsT_scale=zero_scales[:],
+                rhs=picked_words[:, 0 : HALF // 2].bitcast(U8).bitcast(FP4X4),
+                rhs_scale=picked_scales[:].bitcast(U8)[:, 0:HALF],
+                start=True,
+                stop=True,
+            )
         gather_words(1)
         part_words(0, "v_codes0")
         cast(("g", 0), 0, nc.scalar.copy)
@@ -157,7 +175,8 @@ def tile_list_gmlpt_tanh_res_none_kernel(
         quantize_weight(("g", 0), 1)
         cast(("g", 1), 0, nc.scalar.copy)
         cast(("g", 1), 1, nc.vector.tensor_copy)
-        quantize_whole(("g", 1))
+        quantize_weight(("g", 1), 1)
+        quantize_weight(("g", 1), 0)
         cast(("u", 0), 0, nc.vector.tensor_copy)
         cast(("u", 0), 1, nc.vector.tensor_copy)
         quantize_whole(("u", 0))
@@ -170,11 +189,10 @@ def tile_list_gmlpt_tanh_res_none_kernel(
         def new_bank(i):
             return psum.tile([P, HALF], F32, name="bank%d" % i)
 
-        gate_first = keep.tile([P, 3 * CHUNK * PACK], F32, name="gate_first")
-        gate_rest = keep.tile([P, 5 * CHUNK * PACK], F32, name="gate_rest", tag="raw_u1")
-        gate_chunks = ((gate_first, 0), (gate_first, 1), (gate_first, 2), (gate_rest, 0))
-        gate_rows = gate_rest[:, CHUNK * PACK :].rearrange("p (t j) -> p t j", t=PACK)
-        gate_banks = [new_bank(i) for i in range(2 * PACK)]
+        gate_first = keep.tile([P, EARLY * CHUNK * PACK], F32, name="gate_first")
+        gate_rest = keep.tile([P, (CHUNKS - EARLY) * CHUNK * PACK], F32, name="gate_rest", tag="raw_u1")
+        gate_chunks = [(gate_first, c) if c < EARLY else (gate_rest, c - EARLY) for c in range(CHUNKS)]
+        gate_banks = [new_bank(i) for i in range(CHUNKS)]
 
         def token_major(bank):
             return bank[:].rearrange("p (t j) -> p j t", t=PACK)
@@ -185,21 +203,20 @@ def tile_list_gmlpt_tanh_res_none_kernel(
         def gate_chunk(c, a, tiles):
             for t in tiles:
                 acc = gate_banks[c][:, t * CHUNK : (t + 1) * CHUNK]
-                first_layer_pass(acc, ("g", a), t, c * CHUNK, CHUNK, a == 0 and t == 0, a == 1 and t == PACK - 1)
+                first_layer_pass(acc, ("g", a), t, c * CHUNK, CHUNK, a == 0 and t == 0, a == 1 and t == 1)
+
+        def gate_tanh(c):
+            nc.scalar.activation(chunk_of(*gate_chunks[c]), token_major(gate_banks[c]), TANH, bias=warm_out[:, 0:1])
 
         for u in range(2):
-            for c in range(4):
+            for c in range(CHUNKS):
                 gate_chunk(c, 0, (2 * u, 2 * u + 1))
-            for t in (2 * u, 2 * u + 1):
-                first_layer_pass(gate_banks[PACK + t][:], ("g", 0), t, HALF, HALF, True, False)
-        for c in range(4):
-            gate_chunk(c, 1, range(PACK))
-        for t in range(PACK):
-            first_layer_pass(gate_banks[PACK + t][:], ("g", 1), t, HALF, HALF, False, True)
-        for c in range(4):
-            nc.scalar.activation(chunk_of(*gate_chunks[c]), token_major(gate_banks[c]), TANH, bias=warm_out[:, 0:1])
-        for t in range(PACK):
-            nc.scalar.activation(gate_rows[:, t, :], gate_banks[PACK + t][:], TANH, bias=warm_out[:, 0:1])
+        for h in range(2):
+            for tiles in ((2, 3), (0, 1)):
+                for c in range(4 * h, 4 * h + 4):
+                    gate_chunk(c, 1, tiles)
+        for c in range(6):
+            gate_tanh(c)
 
         hidden = keep.tile([P, J * PACK], BF16, name="hidden", align_bytes=64)
         h_codes = keep.tile([P, J], U32, name="h_codes", align_bytes=64)
@@ -218,17 +235,7 @@ def tile_list_gmlpt_tanh_res_none_kernel(
                 first_layer_pass(acc, ("u", a), t, c * CHUNK, CHUNK, opens and t == 0, not opens and t == PACK - 1)
 
         def up_and_multiply(c):
-            j0 = c * CHUNK
-            bank = up_banks[c]
-            if c < 4:
-                nc.vector.tensor_tensor(chunk_of(hidden, c), token_major(bank), chunk_of(*gate_chunks[c]), MULT)
-                return
-            nc.vector.tensor_tensor(
-                hidden[:, j0 * PACK : (j0 + CHUNK) * PACK].rearrange("p (c e t) -> p c t e", e=2, t=PACK),
-                bank[:].rearrange("p (t c e) -> p c t e", t=PACK, e=2),
-                gate_rows[:, :, j0 % HALF : j0 % HALF + CHUNK].rearrange("p t (c e) -> p c t e", e=2),
-                MULT,
-            )
+            nc.vector.tensor_tensor(chunk_of(hidden, c), token_major(up_banks[c]), chunk_of(*gate_chunks[c]), MULT)
 
         def quantize_hidden(j0, width):
             nc.vector.quantize_mx(
@@ -305,34 +312,37 @@ def tile_list_gmlpt_tanh_res_none_kernel(
             up_passes(c, 1, True)
             up_passes(c, 0, False)
 
-        for c in range(EARLY):
+        for c in range(4):
             up_passes(c, 0, True)
-        for c in range(EARLY):
+        for c in range(4):
             up_passes(c, 1, False)
-        up_both(3)
-        up_both(4)
-        up_both(5)
+        up_rows = keep.tile([P, CHUNK * PACK], F32, name="up_rows")
+        nc.scalar.copy(chunk_of(up_rows, 0), token_major(up_banks[1]))
+        nc.gpsimd.tensor_tensor(
+            hidden[:, CHUNK * PACK : 2 * CHUNK * PACK], up_rows[:], gate_first[:, CHUNK * PACK : 2 * CHUNK * PACK], MULT
+        )
+        for c in range(6, CHUNKS):
+            gate_tanh(c)
+        for c in range(4, CHUNKS):
+            up_both(c)
         up_and_multiply(0)
-        up_and_multiply(1)
         up_and_multiply(2)
-        quantize_hidden(0, 2 * CHUNK)
-        down_pair(0, 0)
         up_and_multiply(3)
-        up_both(6)
         up_and_multiply(4)
-        up_both(7)
         quantize_hidden(2 * CHUNK, 2 * CHUNK)
-        down_pair(2, 1)
+        down_pair(2, 0)
         up_and_multiply(5)
+        quantize_hidden(0, 2 * CHUNK)
+        down_pair(0, 1)
         quantize_hidden(4 * CHUNK, CHUNK)
         down_chunk(4, 2, nc.scalar.copy)
         up_and_multiply(6)
         quantize_hidden(5 * CHUNK, CHUNK)
-        down_chunk(5, 6, nc.scalar.copy)
+        down_chunk(5, 3, nc.scalar.copy)
         store(0, 2, 4 * CHUNK, 2 * CHUNK)
         up_and_multiply(7)
         quantize_hidden(6 * CHUNK, CHUNK)
         quantize_hidden(7 * CHUNK, CHUNK)
-        down_chunk(6, 7, nc.scalar.copy)
+        down_chunk(6, 4, nc.scalar.copy)
         store(0, 2, 6 * CHUNK, CHUNK)
-        down_by_rows(7 * CHUNK, CHUNK, (5, 0), (nc.scalar.copy, nc.vector.tensor_copy))
+        down_by_rows(7 * CHUNK, CHUNK, (5, 6), (nc.scalar.copy, nc.vector.tensor_copy))

@@ -280,14 +280,14 @@ def tile_list_gmlpt_tanh_res_none_kernel(
                 down_group(bank[:, b * CHUNK : (b + 1) * CHUNK], b, j0, CHUNK)
             copy(result[:, :, j0 : j0 + CHUNK], bank[:, 0 : 2 * CHUNK].rearrange("p (b j) -> p b j", b=N // P))
 
-        def down_pair(c, i):
+        def down_pair(c, banks):
             j0 = c * CHUNK
-            bank = new_bank(i)
             for b in range(N // P):
+                bank = new_bank(banks[b])
                 for e in range(2):
                     cols = slice(j0 + e * CHUNK, j0 + (e + 1) * CHUNK)
                     nc.tensor.matmul_mx(
-                        out=bank[:, (2 * b + e) * CHUNK : (2 * b + e + 1) * CHUNK],
+                        out=bank[:, e * CHUNK : (e + 1) * CHUNK],
                         lhsT=wd4_codes[:].bitcast(U8)[:, 2 * b * P : 2 * (b + 1) * P].bitcast(FP4X4),
                         lhsT_scale=wd_planes[:, 0, b * P : (b + 1) * P],
                         rhs=h_codes[:, cols].bitcast(FP8X4),
@@ -297,7 +297,7 @@ def tile_list_gmlpt_tanh_res_none_kernel(
                     )
                 cols = slice(j0, j0 + 2 * CHUNK)
                 nc.tensor.matmul_mx(
-                    out=bank[:, 2 * b * CHUNK : 2 * (b + 1) * CHUNK],
+                    out=bank[:, 0 : 2 * CHUNK],
                     lhsT=wd8_codes[:, b * P : (b + 1) * P].bitcast(FP8X4),
                     lhsT_scale=wd_planes[:, 1, b * P : (b + 1) * P],
                     rhs=h_codes[:, cols].bitcast(FP8X4),
@@ -305,8 +305,8 @@ def tile_list_gmlpt_tanh_res_none_kernel(
                     start=False,
                     stop=True,
                 )
-            nc.scalar.copy(result[:, :, j0 : j0 + 2 * CHUNK], bank[:].rearrange("p (b j) -> p b j", b=N // P))
-            store(0, 2, j0, 2 * CHUNK)
+                nc.scalar.copy(result[:, b, cols], bank[:, 0 : 2 * CHUNK])
+                store(b, b + 1, j0, 2 * CHUNK)
 
         def up_both(c):
             up_passes(c, 1, True)
@@ -330,19 +330,19 @@ def tile_list_gmlpt_tanh_res_none_kernel(
         up_and_multiply(3)
         up_and_multiply(4)
         quantize_hidden(2 * CHUNK, 2 * CHUNK)
-        down_pair(2, 0)
+        down_pair(2, (0, 1))
         up_and_multiply(5)
         quantize_hidden(0, 2 * CHUNK)
-        down_pair(0, 1)
+        down_pair(0, (2, 3))
         quantize_hidden(4 * CHUNK, CHUNK)
-        down_chunk(4, 2, nc.scalar.copy)
+        down_chunk(4, 4, nc.scalar.copy)
         up_and_multiply(6)
         quantize_hidden(5 * CHUNK, CHUNK)
-        down_chunk(5, 3, nc.scalar.copy)
+        down_chunk(5, 5, nc.scalar.copy)
         store(0, 2, 4 * CHUNK, 2 * CHUNK)
         up_and_multiply(7)
         quantize_hidden(6 * CHUNK, CHUNK)
         quantize_hidden(7 * CHUNK, CHUNK)
-        down_chunk(6, 4, nc.scalar.copy)
+        down_chunk(6, 0, nc.vector.tensor_copy)
         store(0, 2, 6 * CHUNK, CHUNK)
-        down_by_rows(7 * CHUNK, CHUNK, (5, 6), (nc.scalar.copy, nc.vector.tensor_copy))
+        down_by_rows(7 * CHUNK, CHUNK, (1, 6), (nc.scalar.copy, nc.scalar.copy))

@@ -26,7 +26,7 @@ ROW0 = 96
 CHUNKS = J // CHUNK
 WARM_PASSES = 4
 EARLY = 4
-SHARE = 256
+SHARE = 192
 UP_BANKS = (0, 1, 2, 3, 4, 5, 6, 7)
 
 
@@ -227,10 +227,10 @@ def tile_list_gmlpt_tanh_res_none_kernel(
 
         up_banks = {}
 
-        def up_passes(c, a, opens):
+        def up_passes(c, a, opens, tiles=range(PACK)):
             if opens:
                 up_banks[c] = new_bank(UP_BANKS[c])
-            for t in range(PACK):
+            for t in tiles:
                 acc = up_banks[c][:, t * CHUNK : (t + 1) * CHUNK]
                 first_layer_pass(acc, ("u", a), t, c * CHUNK, CHUNK, opens and t == 0, not opens and t == PACK - 1)
 
@@ -265,13 +265,6 @@ def tile_list_gmlpt_tanh_res_none_kernel(
 
         def store(b0, b1, j0, width):
             nc.sync.dma_start(out_rows[:, b0:b1, j0 : j0 + width], result[:, b0:b1, j0 : j0 + width])
-
-        def down_by_rows(j0, width, banks, copies):
-            for b in range(N // P):
-                bank = new_bank(banks[b])
-                down_group(bank[:, 0:width], b, j0, width)
-                copies[b](result[:, b, j0 : j0 + width], bank[:, 0:width])
-                store(b, b + 1, j0, width)
 
         def down_chunk(c, i, copy):
             j0 = c * CHUNK
@@ -314,7 +307,10 @@ def tile_list_gmlpt_tanh_res_none_kernel(
 
         for c in range(4):
             up_passes(c, 0, True)
-        for c in range(4):
+        for tiles in ((0, 1), (2, 3)):
+            for c in range(2):
+                up_passes(c, 1, False, tiles)
+        for c in range(2, 4):
             up_passes(c, 1, False)
         up_rows = keep.tile([P, CHUNK * PACK], F32, name="up_rows")
         nc.scalar.copy(chunk_of(up_rows, 0), token_major(up_banks[1]))
@@ -345,4 +341,8 @@ def tile_list_gmlpt_tanh_res_none_kernel(
         quantize_hidden(7 * CHUNK, CHUNK)
         down_chunk(6, 0, nc.vector.tensor_copy)
         store(0, 2, 6 * CHUNK, CHUNK)
-        down_by_rows(7 * CHUNK, CHUNK, (1, 6), (nc.scalar.copy, nc.scalar.copy))
+        for b, i in enumerate((1, 6)):
+            bank = new_bank(i)
+            down_group(bank[:, 0:CHUNK], b, 7 * CHUNK, CHUNK)
+            nc.scalar.copy(result[:, b, 7 * CHUNK : J], bank[:, 0:CHUNK])
+        store(0, 2, 7 * CHUNK, CHUNK)

@@ -25,9 +25,9 @@ CHUNK = 128
 ROW0 = 96
 CHUNKS = J // CHUNK
 WARM_PASSES = 4
-EARLY = 4
-SHARE = 192
-UP_BANKS = (0, 1, 2, 3, 4, 5, 6, 7)
+QUARTER = 256
+ASIDE = 2
+SHARE = 128
 
 
 def tile_list_gmlpt_tanh_res_none_kernel(
@@ -47,24 +47,25 @@ def tile_list_gmlpt_tanh_res_none_kernel(
         wd4_codes = keep.tile([P, 2 * N // 4], I32, name="wd4_codes", align_bytes=64)
         wd8_codes = keep.tile([P, N], I32, name="wd8_codes", align_bytes=64)
         wd_scales = keep.tile([P, 2, N // 4], I32, name="wd_scales", align_bytes=64)
-        warm = keep.tile([P, 8], F32, name="warm")
         warm_out = keep.tile([P, 8], F32, name="warm_out")
 
         nc.vector.memset(wd_scales[:], 0)
         nc.vector.memset(scale_window[0:ROW0, :], 0)
-        nc.vector.memset(warm[:], 0.0)
         nc.vector.memset(moved_scales[0][:], 0)
         nc.vector.memset(moved_scales[1][:], 0)
-        zeros = keep.tile([P, K_PASS], BF16, name="zeros", align_bytes=64)
-        zero_codes = keep.tile([P, P], U32, name="zero_codes", align_bytes=64)
-        zero_scales = keep.tile([P, P], U8, name="zero_scales", align_bytes=64)
-        nc.vector.memset(zeros[:], 0.0)
-        nc.vector.quantize_mx(out=zero_codes[:].bitcast(FP8X4), scales=zero_scales[:], in_=zeros[:])
+        zeros = keep.tile([P, 5 * P], I32, name="zeros", align_bytes=64)
+        nc.vector.memset(zeros[:], 0)
+        zero_codes = zeros[:, 0 : 2 * P]
+        zero_scales = zeros[:, 2 * P : 3 * P].bitcast(U8)
+        zero_values = zeros[:, 3 * P : 5 * P]
+        nc.vector.quantize_mx(
+            out=zero_codes[:, 0:P].bitcast(FP8X4), scales=zero_scales[:, 0:P], in_=zero_values.bitcast(BF16)
+        )
 
         nc.sync.dma_start(scale_window[ROW0:P, :], tab_scales.bitcast(I32).rearrange("a q t -> (a q) t"))
         nc.sync.dma_start(offsets[:], offs)
         nc.sync.dma_start(word_window[:], tab_words[0].rearrange("p t b -> p (t b)").bitcast(I32))
-        nc.scalar.activation(warm_out[:], warm[:], TANH)
+        nc.scalar.activation(warm_out[:], zero_values[:, 0:8].bitcast(F32), TANH)
 
         def load_down_scales(f, scales):
             rows = scales[0].bitcast(I32).rearrange("(q r) n -> r q n", r=4)
@@ -97,15 +98,11 @@ def tile_list_gmlpt_tanh_res_none_kernel(
 
         load_down_scales(1, wd8_scales)
 
-        grouped, whole, w_codes, w_scales, v_codes = {}, {}, {}, {}, {}
+        grouped, w_codes, w_scales, v_codes = {}, {}, {}, {}
         for key in raw:
-            if key == ("u", 0):
-                whole[key] = keep.tile([P, PACK, P * PACK], BF16, name="staging_%s%d" % key, align_bytes=64)
-                grouped[key, 0], grouped[key, 1] = whole[key][:, 0:2], whole[key][:, 2:4]
-            else:
-                for u in range(2):
-                    tag = "staging_%s%d%d" % (key[0], key[1], u)
-                    grouped[key, u] = keep.tile([P, 2, P * PACK], BF16, name=tag, tag=tag, align_bytes=64)
+            for u in range(2):
+                tag = "staging_%s%d%d" % (key[0], key[1], u)
+                grouped[key, u] = keep.tile([P, 2, P * PACK], BF16, name=tag, tag=tag, align_bytes=64)
             w_codes[key] = keep.tile([P, R], U32, name="w_codes_%s%d" % key, align_bytes=64)
             w_scales[key] = keep.tile([P, R], U8, name="w_scales_%s%d" % key, align_bytes=64)
 
@@ -120,13 +117,6 @@ def tile_list_gmlpt_tanh_res_none_kernel(
                 out=w_codes[key][:, cols].bitcast(FP8X4),
                 scales=w_scales[key][:, cols],
                 in_=grouped[key, u][:].rearrange("p e x -> p (e x)"),
-            )
-
-        def quantize_whole(key):
-            nc.vector.quantize_mx(
-                out=w_codes[key][:].bitcast(FP8X4),
-                scales=w_scales[key][:],
-                in_=whole[key][:].rearrange("p t x -> p (t x)"),
             )
 
         def gather_words(h):
@@ -159,10 +149,10 @@ def tile_list_gmlpt_tanh_res_none_kernel(
         for i in range(WARM_PASSES):
             nc.tensor.matmul_mx(
                 out=idle_bank[:],
-                lhsT=zero_codes[:].bitcast(FP8X4),
-                lhsT_scale=zero_scales[:],
-                rhs=picked_words[:, 0 : HALF // 2].bitcast(U8).bitcast(FP4X4),
-                rhs_scale=picked_scales[:].bitcast(U8)[:, 0:HALF],
+                lhsT=zero_codes[:, 0:P].bitcast(FP8X4),
+                lhsT_scale=wd_scales[:, 0, :].bitcast(U8)[:, 0:P],
+                rhs=zero_codes.bitcast(U8).bitcast(FP4X4),
+                rhs_scale=zero_scales,
                 start=True,
                 stop=True,
             )
@@ -179,7 +169,8 @@ def tile_list_gmlpt_tanh_res_none_kernel(
         quantize_weight(("g", 1), 0)
         cast(("u", 0), 0, nc.vector.tensor_copy)
         cast(("u", 0), 1, nc.vector.tensor_copy)
-        quantize_whole(("u", 0))
+        quantize_weight(("u", 0), 0)
+        quantize_weight(("u", 0), 1)
         cast(("u", 1), 0, nc.vector.tensor_copy)
         cast(("u", 1), 1, nc.vector.tensor_copy, 0, SHARE)
         cast(("u", 1), 1, nc.scalar.copy, SHARE, R)
@@ -189,34 +180,35 @@ def tile_list_gmlpt_tanh_res_none_kernel(
         def new_bank(i):
             return psum.tile([P, HALF], F32, name="bank%d" % i)
 
-        gate_first = keep.tile([P, EARLY * CHUNK * PACK], F32, name="gate_first")
-        gate_rest = keep.tile([P, (CHUNKS - EARLY) * CHUNK * PACK], F32, name="gate_rest", tag="raw_u1")
-        gate_chunks = [(gate_first, c) if c < EARLY else (gate_rest, c - EARLY) for c in range(CHUNKS)]
-        gate_banks = [new_bank(i) for i in range(CHUNKS)]
-
         def token_major(bank):
             return bank[:].rearrange("p (t j) -> p j t", t=PACK)
 
         def chunk_of(tile, c):
             return tile[:, c * CHUNK * PACK : (c + 1) * CHUNK * PACK].rearrange("p (j t) -> p j t", t=PACK)
 
-        def gate_chunk(c, a, tiles):
-            for t in tiles:
-                acc = gate_banks[c][:, t * CHUNK : (t + 1) * CHUNK]
-                first_layer_pass(acc, ("g", a), t, c * CHUNK, CHUNK, a == 0 and t == 0, a == 1 and t == 1)
+        late = keep.tile([P, 2, 2 * QUARTER * 2], F32, name="gate_late", tag="raw_u1")
+        soon = keep.tile([P, 2, 2 * QUARTER * 2], F32, name="gate_soon")
+        gate_pairs = (soon[:, 0], soon[:, 1], late[:, 0], late[:, 1])
+        gate_order = ((1, 0), (1, 1), (0, 0), (0, 1), (1, 2), (0, 2), (1, 3), (0, 3))
+        gate_banks = {key: new_bank(i) for i, key in enumerate(gate_order)}
 
-        def gate_tanh(c):
-            nc.scalar.activation(chunk_of(*gate_chunks[c]), token_major(gate_banks[c]), TANH, bias=warm_out[:, 0:1])
+        def gate_passes(u, q, a):
+            for e in range(2):
+                acc = gate_banks[u, q][:, e * QUARTER : (e + 1) * QUARTER]
+                first_layer_pass(acc, ("g", a), 2 * u + e, q * QUARTER, QUARTER, a == 0 and e == 0, a == 1 and e == 1)
+
+        def gate_tanh(u, q):
+            dst = gate_pairs[q][:, u * QUARTER * 2 : (u + 1) * QUARTER * 2].rearrange("p (j e) -> p j e", e=2)
+            src = gate_banks[u, q][:].rearrange("p (e j) -> p j e", e=2)
+            nc.scalar.activation(dst, src, TANH, bias=warm_out[:, 0:1])
 
         for u in range(2):
-            for c in range(CHUNKS):
-                gate_chunk(c, 0, (2 * u, 2 * u + 1))
-        for h in range(2):
-            for tiles in ((2, 3), (0, 1)):
-                for c in range(4 * h, 4 * h + 4):
-                    gate_chunk(c, 1, tiles)
-        for c in range(6):
-            gate_tanh(c)
+            for q in range(4):
+                gate_passes(u, q, 0)
+        for u, q in gate_order:
+            gate_passes(u, q, 1)
+        for u, q in gate_order[:6]:
+            gate_tanh(u, q)
 
         hidden = keep.tile([P, J * PACK], BF16, name="hidden", align_bytes=64)
         h_codes = keep.tile([P, J], U32, name="h_codes", align_bytes=64)
@@ -227,15 +219,26 @@ def tile_list_gmlpt_tanh_res_none_kernel(
 
         up_banks = {}
 
-        def up_passes(c, a, opens, tiles=range(PACK)):
-            if opens:
-                up_banks[c] = new_bank(UP_BANKS[c])
+        def up_passes(c, a, tiles, first=None, last=None):
             for t in tiles:
                 acc = up_banks[c][:, t * CHUNK : (t + 1) * CHUNK]
-                first_layer_pass(acc, ("u", a), t, c * CHUNK, CHUNK, opens and t == 0, not opens and t == PACK - 1)
+                first_layer_pass(acc, ("u", a), t, c * CHUNK, CHUNK, t == first, t == last)
 
-        def up_and_multiply(c):
-            nc.vector.tensor_tensor(chunk_of(hidden, c), token_major(up_banks[c]), chunk_of(*gate_chunks[c]), MULT)
+        def up_both(c, i):
+            up_banks[c] = new_bank(i)
+            up_passes(c, 1, (2, 3, 0, 1), first=2)
+            up_passes(c, 0, (0, 1, 2, 3), last=3)
+
+        def by_pairs(tile, c):
+            return tile[:, c * CHUNK * PACK : (c + 1) * CHUNK * PACK].rearrange("p (j u e) -> p j u e", u=2, e=2)
+
+        def gate_of(c):
+            j0 = (c % 2) * CHUNK
+            return gate_pairs[c // 2].rearrange("p (u j e) -> p j u e", u=2, e=2)[:, j0 : j0 + CHUNK]
+
+        def multiply(c):
+            src = up_banks[c][:].rearrange("p (u e j) -> p j u e", u=2, e=2)
+            nc.vector.tensor_tensor(by_pairs(hidden, c), src, gate_of(c), MULT)
 
         def quantize_hidden(j0, width):
             nc.vector.quantize_mx(
@@ -277,71 +280,53 @@ def tile_list_gmlpt_tanh_res_none_kernel(
             j0 = c * CHUNK
             for b in range(N // P):
                 bank = new_bank(banks[b])
-                for e in range(2):
-                    cols = slice(j0 + e * CHUNK, j0 + (e + 1) * CHUNK)
-                    nc.tensor.matmul_mx(
-                        out=bank[:, e * CHUNK : (e + 1) * CHUNK],
-                        lhsT=wd4_codes[:].bitcast(U8)[:, 2 * b * P : 2 * (b + 1) * P].bitcast(FP4X4),
-                        lhsT_scale=wd_planes[:, 0, b * P : (b + 1) * P],
-                        rhs=h_codes[:, cols].bitcast(FP8X4),
-                        rhs_scale=h_scales[:, cols],
-                        start=e == 0,
-                        stop=False,
-                    )
-                cols = slice(j0, j0 + 2 * CHUNK)
-                nc.tensor.matmul_mx(
-                    out=bank[:, 0 : 2 * CHUNK],
-                    lhsT=wd8_codes[:, b * P : (b + 1) * P].bitcast(FP8X4),
-                    lhsT_scale=wd_planes[:, 1, b * P : (b + 1) * P],
-                    rhs=h_codes[:, cols].bitcast(FP8X4),
-                    rhs_scale=h_scales[:, cols],
-                    start=False,
-                    stop=True,
-                )
-                nc.scalar.copy(result[:, b, cols], bank[:, 0 : 2 * CHUNK])
+                down_group(bank[:, 0 : 2 * CHUNK], b, j0, 2 * CHUNK)
+                nc.scalar.copy(result[:, b, j0 : j0 + 2 * CHUNK], bank[:, 0 : 2 * CHUNK])
                 store(b, b + 1, j0, 2 * CHUNK)
 
-        def up_both(c):
-            up_passes(c, 1, True)
-            up_passes(c, 0, False)
-
-        for c in range(4):
-            up_passes(c, 0, True)
+        early = (0, ASIDE, 1, 3)
+        for i, c in enumerate(early):
+            up_banks[c] = new_bank(i)
         for tiles in ((0, 1), (2, 3)):
-            for c in range(2):
-                up_passes(c, 1, False, tiles)
-        for c in range(2, 4):
-            up_passes(c, 1, False)
+            for c in early[:2]:
+                up_passes(c, 0, tiles, first=0)
+        for c in early[2:]:
+            up_passes(c, 0, (0, 1, 2, 3), first=0)
+        for tiles in ((0, 1), (2, 3)):
+            for c in early[:2]:
+                up_passes(c, 1, tiles, last=3)
+        for c in early[2:]:
+            up_passes(c, 1, (2, 3, 0, 1), last=1)
         up_rows = keep.tile([P, CHUNK * PACK], F32, name="up_rows")
-        nc.scalar.copy(chunk_of(up_rows, 0), token_major(up_banks[1]))
-        nc.gpsimd.tensor_tensor(
-            hidden[:, CHUNK * PACK : 2 * CHUNK * PACK], up_rows[:], gate_first[:, CHUNK * PACK : 2 * CHUNK * PACK], MULT
-        )
-        for c in range(6, CHUNKS):
-            gate_tanh(c)
-        for c in range(4, CHUNKS):
-            up_both(c)
-        up_and_multiply(0)
-        up_and_multiply(2)
-        up_and_multiply(3)
-        up_and_multiply(4)
-        quantize_hidden(2 * CHUNK, 2 * CHUNK)
-        down_pair(2, (0, 1))
-        up_and_multiply(5)
+        nc.scalar.copy(chunk_of(up_rows, 0), token_major(up_banks[ASIDE]))
+        nc.gpsimd.tensor_tensor(by_pairs(hidden, ASIDE), by_pairs(up_rows, 0), gate_of(ASIDE), MULT)
+        for u, q in gate_order[6:]:
+            gate_tanh(u, q)
+        up_both(4, 4)
+        up_both(5, 5)
+        up_both(6, 1)
+        multiply(0)
+        multiply(1)
+        multiply(3)
         quantize_hidden(0, 2 * CHUNK)
-        down_pair(0, (2, 3))
+        down_pair(0, (0, 6))
+        up_both(7, 0)
+        multiply(4)
+        quantize_hidden(2 * CHUNK, 2 * CHUNK)
+        down_pair(2, (2, 7))
+        multiply(5)
         quantize_hidden(4 * CHUNK, CHUNK)
-        down_chunk(4, 4, nc.scalar.copy)
-        up_and_multiply(6)
+        down_chunk(4, 3, nc.scalar.copy)
+        multiply(6)
         quantize_hidden(5 * CHUNK, CHUNK)
-        down_chunk(5, 5, nc.scalar.copy)
+        down_chunk(5, 4, nc.scalar.copy)
         store(0, 2, 4 * CHUNK, 2 * CHUNK)
-        up_and_multiply(7)
+        multiply(7)
         quantize_hidden(6 * CHUNK, CHUNK)
         quantize_hidden(7 * CHUNK, CHUNK)
-        down_chunk(6, 0, nc.vector.tensor_copy)
+        down_chunk(6, 5, nc.vector.tensor_copy)
         store(0, 2, 6 * CHUNK, CHUNK)
-        for b, i in enumerate((1, 6)):
+        for b, i in enumerate((6, 1)):
             bank = new_bank(i)
             down_group(bank[:, 0:CHUNK], b, 7 * CHUNK, CHUNK)
             nc.scalar.copy(result[:, b, 7 * CHUNK : J], bank[:, 0:CHUNK])

@@ -39,7 +39,7 @@ def tile_list_gmlpt_tanh_res_none_kernel(
         psum = ctx.enter_context(tc.psum_pool(name="psum", bufs=1))
 
         offsets = keep.tile([P, J // 16], U16, name="offsets")
-        scale_window = keep.tile([P, T // 4], I32, name="scale_window", align_bytes=64)
+        scale_window = keep.tile([P, T // 4], I32, name="scale_window", tag="scale_window", align_bytes=64)
         word_window = keep.tile([P, T], I32, name="word_window", align_bytes=64)
         picked_scales = keep.tile([P, J // 4], I32, name="picked_scales", align_bytes=64)
         moved_scales = [keep.tile([P, J // 4], I32, name="moved_scales%d" % a, align_bytes=64) for a in range(PASSES)]
@@ -67,12 +67,12 @@ def tile_list_gmlpt_tanh_res_none_kernel(
         nc.sync.dma_start(word_window[:], tab_words[0].rearrange("p t b -> p (t b)").bitcast(I32))
         nc.scalar.activation(warm_out[:], zero_values[:, 0:8].bitcast(F32), TANH)
 
-        def load_down_scales(f, scales):
+        def load_down_scales(f, scales, which):
             rows = scales[0].bitcast(I32).rearrange("(q r) n -> r q n", r=4)
-            for r in range(4):
+            for r in which:
                 nc.sync.dma_start(wd_scales[r:P:32, f, :], rows[r])
 
-        load_down_scales(0, wd4_scales)
+        load_down_scales(0, wd4_scales, range(3))
         raw = {}
 
         def load_weight(name, w, a, pieces):
@@ -87,7 +87,12 @@ def tile_list_gmlpt_tanh_res_none_kernel(
                 nc.sync.dma_start(moved_scales[a][32 * q : 32 * q + 4, :], picked_scales[first : first + 4, :])
 
         load_weight("g", wg, 0, ((0, R),))
+        load_down_scales(0, wd4_scales, (3,))
         nc.vector.tensor_copy(picked_scales[:].bitcast(U8), scale_window[:].bitcast(U8).indirect(offsets[:]))
+        idle = keep.tile([P, P + P // 4], I32, name="idle", tag="scale_window", align_bytes=64)
+        idle_codes = idle[:, 0:P].bitcast(FP8X4)
+        idle_scales = idle[:, P:].bitcast(U8)
+        nc.vector.quantize_mx(out=idle_codes, scales=idle_scales, in_=zero_values.bitcast(BF16))
         move_scales(0)
         load_weight("g", wg, 1, ((0, R),))
         move_scales(1)
@@ -96,7 +101,7 @@ def tile_list_gmlpt_tanh_res_none_kernel(
         nc.sync.dma_start(wd4_codes[:], wd4_words[0].bitcast(I32))
         nc.sync.dma_start(wd8_codes[:], wd8_words[0].rearrange("p n b -> p (n b)").bitcast(I32))
 
-        load_down_scales(1, wd8_scales)
+        load_down_scales(1, wd8_scales, range(4))
 
         grouped, w_codes, w_scales, v_codes = {}, {}, {}, {}
         for key in raw:
@@ -149,8 +154,8 @@ def tile_list_gmlpt_tanh_res_none_kernel(
         for i in range(WARM_PASSES):
             nc.tensor.matmul_mx(
                 out=idle_bank[:],
-                lhsT=zero_codes[:, 0:P].bitcast(FP8X4),
-                lhsT_scale=wd_scales[:, 0, :].bitcast(U8)[:, 0:P],
+                lhsT=idle_codes,
+                lhsT_scale=idle_scales if i < WARM_PASSES // 2 else wd_scales[:, 0, :].bitcast(U8)[:, 0:P],
                 rhs=zero_codes.bitcast(U8).bitcast(FP4X4),
                 rhs_scale=zero_scales,
                 start=True,
@@ -304,19 +309,19 @@ def tile_list_gmlpt_tanh_res_none_kernel(
             gate_tanh(u, q)
         up_both(4, 4)
         up_both(5, 5)
-        up_both(6, 1)
+        up_both(6, 6)
         multiply(0)
         multiply(1)
         multiply(3)
-        quantize_hidden(0, 2 * CHUNK)
-        down_pair(0, (0, 6))
-        up_both(7, 0)
         multiply(4)
-        quantize_hidden(2 * CHUNK, 2 * CHUNK)
-        down_pair(2, (2, 7))
+        quantize_hidden(0, 2 * CHUNK)
+        down_pair(0, (0, 1))
         multiply(5)
+        up_both(7, 5)
+        quantize_hidden(2 * CHUNK, 2 * CHUNK)
+        down_pair(2, (2, 3))
         quantize_hidden(4 * CHUNK, CHUNK)
-        down_chunk(4, 3, nc.scalar.copy)
+        down_chunk(4, 7, nc.scalar.copy)
         multiply(6)
         quantize_hidden(5 * CHUNK, CHUNK)
         down_chunk(5, 4, nc.scalar.copy)
@@ -324,9 +329,9 @@ def tile_list_gmlpt_tanh_res_none_kernel(
         multiply(7)
         quantize_hidden(6 * CHUNK, CHUNK)
         quantize_hidden(7 * CHUNK, CHUNK)
-        down_chunk(6, 5, nc.vector.tensor_copy)
+        down_chunk(6, 0, nc.vector.tensor_copy)
         store(0, 2, 6 * CHUNK, CHUNK)
-        for b, i in enumerate((6, 1)):
+        for b, i in enumerate((1, 6)):
             bank = new_bank(i)
             down_group(bank[:, 0:CHUNK], b, 7 * CHUNK, CHUNK)
             nc.scalar.copy(result[:, b, 7 * CHUNK : J], bank[:, 0:CHUNK])

@@ -27,7 +27,7 @@ CHUNKS = J // CHUNK
 WARM_PASSES = 4
 QUARTER = 256
 ASIDE = 2
-SHARE = 128
+SHARE = 160
 
 
 def tile_list_gmlpt_tanh_res_none_kernel(
@@ -130,10 +130,13 @@ def tile_list_gmlpt_tanh_res_none_kernel(
                 word_window[:].bitcast(U32).indirect(offsets[:, h * HALF // 16 : (h + 1) * HALF // 16]),
             )
 
-        def part_words(h, tag):
-            v_codes[h] = keep.tile([P, PASSES, 2 * HALF], U8, name="v_codes%d" % h, tag=tag, align_bytes=64)
-            src = picked_words[:, h * HALF : (h + 1) * HALF].bitcast(U16).rearrange("p (j d) -> p d j", d=2)
-            nc.vector.tensor_copy(v_codes[h][:].bitcast(U16), src)
+        def part_words(q0, q1, tag):
+            width = (q1 - q0) * QUARTER
+            parted = keep.tile([P, PASSES, 2 * width], U8, name="v_codes%d" % q0, tag=tag, align_bytes=64)
+            src = picked_words[:, q0 * QUARTER : q1 * QUARTER].bitcast(U16).rearrange("p (j d) -> p d j", d=2)
+            nc.vector.tensor_copy(parted[:].bitcast(U16), src)
+            for q in range(q0, q1):
+                v_codes[q] = parted[:, :, 2 * (q - q0) * QUARTER : 2 * (q - q0 + 1) * QUARTER]
 
         v_scales = (moved_scales[0][:].bitcast(U8), moved_scales[1][:].bitcast(U8))
 
@@ -143,7 +146,7 @@ def tile_list_gmlpt_tanh_res_none_kernel(
                 out=acc,
                 lhsT=w_codes[key][:, t * P : (t + 1) * P].bitcast(FP8X4),
                 lhsT_scale=w_scales[key][:, t * P : (t + 1) * P],
-                rhs=v_codes[j0 // HALF][:, a, 2 * (j0 % HALF) : 2 * (j0 % HALF + width)].bitcast(FP4X4),
+                rhs=v_codes[j0 // QUARTER][:, a, 2 * (j0 % QUARTER) : 2 * (j0 % QUARTER + width)].bitcast(FP4X4),
                 rhs_scale=v_scales[a][:, j0 : j0 + width],
                 start=start,
                 stop=stop,
@@ -162,16 +165,17 @@ def tile_list_gmlpt_tanh_res_none_kernel(
                 stop=True,
             )
         gather_words(1)
-        part_words(0, "v_codes0")
+        part_words(0, 2, "v_codes0")
         cast(("g", 0), 0, nc.scalar.copy)
         cast(("g", 0), 1, nc.scalar.copy)
         quantize_weight(("g", 0), 0)
-        part_words(1, "staging_g00")
+        part_words(2, 3, "staging_g00")
         quantize_weight(("g", 0), 1)
         cast(("g", 1), 0, nc.scalar.copy)
         cast(("g", 1), 1, nc.vector.tensor_copy)
         quantize_weight(("g", 1), 1)
         quantize_weight(("g", 1), 0)
+        part_words(3, 4, "staging_g10")
         cast(("u", 0), 0, nc.vector.tensor_copy)
         cast(("u", 0), 1, nc.vector.tensor_copy)
         quantize_weight(("u", 0), 0)
@@ -197,10 +201,10 @@ def tile_list_gmlpt_tanh_res_none_kernel(
         gate_order = ((1, 0), (1, 1), (0, 0), (0, 1), (1, 2), (0, 2), (1, 3), (0, 3))
         gate_banks = {key: new_bank(i) for i, key in enumerate(gate_order)}
 
-        def gate_passes(u, q, a):
+        def gate_passes(u, q, a, opens):
             for e in range(2):
                 acc = gate_banks[u, q][:, e * QUARTER : (e + 1) * QUARTER]
-                first_layer_pass(acc, ("g", a), 2 * u + e, q * QUARTER, QUARTER, a == 0 and e == 0, a == 1 and e == 1)
+                first_layer_pass(acc, ("g", a), 2 * u + e, q * QUARTER, QUARTER, opens and e == 0, not opens and e == 1)
 
         def gate_tanh(u, q):
             dst = gate_pairs[q][:, u * QUARTER * 2 : (u + 1) * QUARTER * 2].rearrange("p (j e) -> p j e", e=2)
@@ -208,10 +212,13 @@ def tile_list_gmlpt_tanh_res_none_kernel(
             nc.scalar.activation(dst, src, TANH, bias=warm_out[:, 0:1])
 
         for u in range(2):
-            for q in range(4):
-                gate_passes(u, q, 0)
-        for u, q in gate_order:
-            gate_passes(u, q, 1)
+            for q in range(3):
+                gate_passes(u, q, 0, True)
+        for u, q in gate_order[:6]:
+            gate_passes(u, q, 1, False)
+        for u, q in gate_order[6:]:
+            gate_passes(u, q, 1, True)
+            gate_passes(u, q, 0, False)
         for u, q in gate_order[:6]:
             gate_tanh(u, q)
 
@@ -310,6 +317,7 @@ def tile_list_gmlpt_tanh_res_none_kernel(
         up_both(4, 4)
         up_both(5, 5)
         up_both(6, 6)
+        up_both(7, 7)
         multiply(0)
         multiply(1)
         multiply(3)
@@ -317,14 +325,13 @@ def tile_list_gmlpt_tanh_res_none_kernel(
         quantize_hidden(0, 2 * CHUNK)
         down_pair(0, (0, 1))
         multiply(5)
-        up_both(7, 5)
         quantize_hidden(2 * CHUNK, 2 * CHUNK)
         down_pair(2, (2, 3))
         quantize_hidden(4 * CHUNK, CHUNK)
-        down_chunk(4, 7, nc.scalar.copy)
+        down_chunk(4, 4, nc.scalar.copy)
         multiply(6)
         quantize_hidden(5 * CHUNK, CHUNK)
-        down_chunk(5, 4, nc.scalar.copy)
+        down_chunk(5, 5, nc.scalar.copy)
         store(0, 2, 4 * CHUNK, 2 * CHUNK)
         multiply(7)
         quantize_hidden(6 * CHUNK, CHUNK)

@@ -20,14 +20,19 @@ P = 128
 PACK = 4
 K_PASS = P * PACK
 PASSES = K // K_PASS
+BANK = 512
 HALF = 512
+QUARTER = 256
 CHUNK = 128
 ROW0 = 96
-CHUNKS = J // CHUNK
-WARM_PASSES = 4
-QUARTER = 256
 ASIDE = 2
 SHARE = 160
+RAW_BYTES = PACK * R * 4
+EARLY_PLANE_BYTES = 128
+RAW_G1_AT = EARLY_PLANE_BYTES
+RAW_U0_AT = RAW_G1_AT + RAW_BYTES
+RAW_U1_AT = RAW_U0_AT + RAW_BYTES
+WORD_WINDOW_AT = RAW_U1_AT - 64
 
 
 def tile_list_gmlpt_tanh_res_none_kernel(
@@ -36,71 +41,93 @@ def tile_list_gmlpt_tanh_res_none_kernel(
     nc = tc.nc
     with ExitStack() as ctx:
         keep = ctx.enter_context(tc.tile_pool(name="keep", bufs=1))
+        shared = ctx.enter_context(tc.tile_pool(name="shared", bufs=1))
         psum = ctx.enter_context(tc.psum_pool(name="psum", bufs=1))
 
         offsets = keep.tile([P, J // 16], U16, name="offsets")
-        scale_window = keep.tile([P, T // 4], I32, name="scale_window", tag="scale_window", align_bytes=64)
-        word_window = keep.tile([P, T], I32, name="word_window", align_bytes=64)
+        scale_window = shared.tile([P, T // 4], I32, name="scale_window", align_bytes=64, offset=0)
+        word_window = shared.tile([P, T], I32, name="word_window", align_bytes=64, offset=WORD_WINDOW_AT)
         picked_scales = keep.tile([P, J // 4], I32, name="picked_scales", align_bytes=64)
-        moved_scales = [keep.tile([P, J // 4], I32, name="moved_scales%d" % a, align_bytes=64) for a in range(PASSES)]
         picked_words = keep.tile([P, J], I32, name="picked_words", align_bytes=64)
-        wd4_codes = keep.tile([P, 2 * N // 4], I32, name="wd4_codes", align_bytes=64)
-        wd8_codes = keep.tile([P, N], I32, name="wd8_codes", align_bytes=64)
-        wd_scales = keep.tile([P, 2, N // 4], I32, name="wd_scales", align_bytes=64)
-        warm_out = keep.tile([P, 8], F32, name="warm_out")
+        v_planes = keep.tile([P, PASSES * J // 4], I32, name="v_planes", align_bytes=64)
+        wd_codes = keep.tile([P, N + N // 2], I32, name="wd_codes", align_bytes=64)
+        wd8_codes = wd_codes[:, 0:N]
+        wd4_codes = wd_codes[:, N : N + N // 2]
+        wd_planes = keep.tile([P, N // 2], I32, name="wd_planes", align_bytes=64)
+        zero_column = keep.tile([P, 8], F32, name="zero_column")
+        gate_bias = keep.tile([P, 8], F32, name="gate_bias")
 
-        nc.vector.memset(wd_scales[:], 0)
         nc.vector.memset(scale_window[0:ROW0, :], 0)
-        nc.vector.memset(moved_scales[0][:], 0)
-        nc.vector.memset(moved_scales[1][:], 0)
-        zeros = keep.tile([P, 5 * P], I32, name="zeros", align_bytes=64)
-        nc.vector.memset(zeros[:], 0)
-        zero_codes = zeros[:, 0 : 2 * P]
-        zero_scales = zeros[:, 2 * P : 3 * P].bitcast(U8)
-        zero_values = zeros[:, 3 * P : 5 * P]
-        nc.vector.quantize_mx(
-            out=zero_codes[:, 0:P].bitcast(FP8X4), scales=zero_scales[:, 0:P], in_=zero_values.bitcast(BF16)
-        )
+        nc.vector.memset(wd_planes[:], 0)
+        nc.vector.memset(wd_codes[:], 0)
+        nc.vector.memset(v_planes[:], 0)
+        nc.gpsimd.memset(zero_column[:], 0.0)
+        nc.scalar.activation(gate_bias[:], zero_column[:], TANH)
 
-        nc.sync.dma_start(scale_window[ROW0:P, :], tab_scales.bitcast(I32).rearrange("a q t -> (a q) t"))
-        nc.sync.dma_start(offsets[:], offs)
-        nc.sync.dma_start(word_window[:], tab_words[0].rearrange("p t b -> p (t b)").bitcast(I32))
-        nc.scalar.activation(warm_out[:], zero_values[:, 0:8].bitcast(F32), TANH)
+        raw = {}
+
+        def load_weight(name, w, a, pool, **place):
+            raw[name, a] = pool.tile([P, PACK, R], F32, name="raw_%s%d" % (name, a), **place)
+            rows = w[a * K_PASS : (a + 1) * K_PASS, :].rearrange("(p j) c -> p j c", j=PACK)
+            nc.sync.dma_start(raw[name, a][:], rows)
 
         def load_down_scales(f, scales, which):
             rows = scales[0].bitcast(I32).rearrange("(q r) n -> r q n", r=4)
             for r in which:
-                nc.sync.dma_start(wd_scales[r:P:32, f, :], rows[r])
-
-        load_down_scales(0, wd4_scales, range(3))
-        raw = {}
-
-        def load_weight(name, w, a, pieces):
-            raw[name, a] = keep.tile([P, PACK, R], F32, name="raw_%s%d" % (name, a), tag="raw_%s%d" % (name, a))
-            rows = w[a * K_PASS : (a + 1) * K_PASS, :].rearrange("(p j) c -> p j c", j=PACK)
-            for c0, c1 in pieces:
-                nc.sync.dma_start(raw[name, a][:, :, c0:c1], rows[:, :, c0:c1])
+                nc.sync.dma_start(wd_planes[r:P:32, f * N // 4 : (f + 1) * N // 4], rows[r])
 
         def move_scales(a):
-            for q in range(4):
-                first = ROW0 + 16 * a + 4 * q
-                nc.sync.dma_start(moved_scales[a][32 * q : 32 * q + 4, :], picked_scales[first : first + 4, :])
+            first = ROW0 + 16 * a
+            for r in range(4):
+                nc.sync.dma_start(
+                    v_planes[r:P:32, a * J // 4 : (a + 1) * J // 4], picked_scales[first + r : first + 16 : 4, :]
+                )
 
-        load_weight("g", wg, 0, ((0, R),))
-        load_down_scales(0, wd4_scales, (3,))
+        nc.sync.dma_start(scale_window[ROW0:P, :], tab_scales.bitcast(I32).rearrange("a q t -> (a q) t"))
+        nc.sync.dma_start(offsets[:], offs)
+        nc.sync.dma_start(word_window[:], tab_words[0].rearrange("p t b -> p (t b)").bitcast(I32))
+        load_weight("g", wg, 0, keep)
+        load_down_scales(0, wd4_scales, (0,))
         nc.vector.tensor_copy(picked_scales[:].bitcast(U8), scale_window[:].bitcast(U8).indirect(offsets[:]))
-        idle = keep.tile([P, P + P // 4], I32, name="idle", tag="scale_window", align_bytes=64)
-        idle_codes = idle[:, 0:P].bitcast(FP8X4)
-        idle_scales = idle[:, P:].bitcast(U8)
-        nc.vector.quantize_mx(out=idle_codes, scales=idle_scales, in_=zero_values.bitcast(BF16))
+        early_plane = shared.tile([P, EARLY_PLANE_BYTES // 4], U32, name="early_plane", align_bytes=64, offset=0)
+        nc.scalar.copy(early_plane[:], wd8_codes[:, 0 : EARLY_PLANE_BYTES // 4].bitcast(U32))
         move_scales(0)
-        load_weight("g", wg, 1, ((0, R),))
+        load_weight("g", wg, 1, shared, align_bytes=64, offset=RAW_G1_AT)
         move_scales(1)
-        load_weight("u", wu, 0, ((0, R),))
-        load_weight("u", wu, 1, ((0, R),))
-        nc.sync.dma_start(wd4_codes[:], wd4_words[0].bitcast(I32))
-        nc.sync.dma_start(wd8_codes[:], wd8_words[0].rearrange("p n b -> p (n b)").bitcast(I32))
 
+        def gather_words(h):
+            nc.vector.tensor_copy(
+                picked_words[:, h * HALF : (h + 1) * HALF].bitcast(U32),
+                word_window[:].bitcast(U32).indirect(offsets[:, h * HALF // 16 : (h + 1) * HALF // 16]),
+            )
+
+        gather_words(0)
+        gather_words(1)
+        load_weight("u", wu, 0, shared, align_bytes=64, offset=RAW_U0_AT)
+        load_weight("u", wu, 1, shared, align_bytes=64, offset=RAW_U1_AT)
+
+        def new_bank(i):
+            return psum.tile([P, BANK], F32, name="bank%d" % i)
+
+        idle_bank = new_bank(7)
+        for stationary_plane, moving_plane in (
+            (early_plane[:].bitcast(U8), wd4_codes.bitcast(U8)),
+            (wd4_codes.bitcast(U8)[:, 0:P], wd_planes[:].bitcast(U8)),
+        ):
+            for repeat in range(2):
+                nc.tensor.matmul_mx(
+                    out=idle_bank[:],
+                    lhsT=wd8_codes[:, 0:P].bitcast(FP8X4),
+                    lhsT_scale=stationary_plane,
+                    rhs=wd8_codes.bitcast(U8).bitcast(FP4X4),
+                    rhs_scale=moving_plane,
+                    start=True,
+                    stop=True,
+                )
+
+        nc.sync.dma_start(wd4_codes, wd4_words[0].bitcast(I32))
+        nc.sync.dma_start(wd8_codes, wd8_words[0].rearrange("p n b -> p (n b)").bitcast(I32))
+        load_down_scales(0, wd4_scales, (1, 2, 3))
         load_down_scales(1, wd8_scales, range(4))
 
         grouped, w_codes, w_scales, v_codes = {}, {}, {}, {}
@@ -111,7 +138,7 @@ def tile_list_gmlpt_tanh_res_none_kernel(
             w_codes[key] = keep.tile([P, R], U32, name="w_codes_%s%d" % key, align_bytes=64)
             w_scales[key] = keep.tile([P, R], U8, name="w_scales_%s%d" % key, align_bytes=64)
 
-        def cast(key, u, copy, c0=0, c1=R):
+        def round_weight(key, u, copy, c0=0, c1=R):
             src = raw[key][:, :, c0:c1].rearrange("p j (m u e) -> p u m j e", u=2, e=2)[:, u]
             dst = grouped[key, u][:, :, c0:c1].rearrange("p e (m j) -> p m j e", j=PACK)
             copy(dst, src)
@@ -124,12 +151,6 @@ def tile_list_gmlpt_tanh_res_none_kernel(
                 in_=grouped[key, u][:].rearrange("p e x -> p (e x)"),
             )
 
-        def gather_words(h):
-            nc.vector.tensor_copy(
-                picked_words[:, h * HALF : (h + 1) * HALF].bitcast(U32),
-                word_window[:].bitcast(U32).indirect(offsets[:, h * HALF // 16 : (h + 1) * HALF // 16]),
-            )
-
         def part_words(q0, q1, tag):
             width = (q1 - q0) * QUARTER
             parted = keep.tile([P, PASSES, 2 * width], U8, name="v_codes%d" % q0, tag=tag, align_bytes=64)
@@ -138,7 +159,7 @@ def tile_list_gmlpt_tanh_res_none_kernel(
             for q in range(q0, q1):
                 v_codes[q] = parted[:, :, 2 * (q - q0) * QUARTER : 2 * (q - q0 + 1) * QUARTER]
 
-        v_scales = (moved_scales[0][:].bitcast(U8), moved_scales[1][:].bitcast(U8))
+        v_scales = v_planes[:].bitcast(U8)
 
         def first_layer_pass(acc, key, t, j0, width, start, stop):
             a = key[1]
@@ -147,55 +168,33 @@ def tile_list_gmlpt_tanh_res_none_kernel(
                 lhsT=w_codes[key][:, t * P : (t + 1) * P].bitcast(FP8X4),
                 lhsT_scale=w_scales[key][:, t * P : (t + 1) * P],
                 rhs=v_codes[j0 // QUARTER][:, a, 2 * (j0 % QUARTER) : 2 * (j0 % QUARTER + width)].bitcast(FP4X4),
-                rhs_scale=v_scales[a][:, j0 : j0 + width],
+                rhs_scale=v_scales[:, a * J + j0 : a * J + j0 + width],
                 start=start,
                 stop=stop,
             )
 
-        gather_words(0)
-        idle_bank = psum.tile([P, HALF], F32, name="bank7")
-        for i in range(WARM_PASSES):
-            nc.tensor.matmul_mx(
-                out=idle_bank[:],
-                lhsT=idle_codes,
-                lhsT_scale=idle_scales if i < WARM_PASSES // 2 else wd_scales[:, 0, :].bitcast(U8)[:, 0:P],
-                rhs=zero_codes.bitcast(U8).bitcast(FP4X4),
-                rhs_scale=zero_scales,
-                start=True,
-                stop=True,
-            )
-        gather_words(1)
         part_words(0, 2, "v_codes0")
-        cast(("g", 0), 0, nc.scalar.copy)
-        cast(("g", 0), 1, nc.scalar.copy)
+        round_weight(("g", 0), 0, nc.scalar.copy)
+        round_weight(("g", 0), 1, nc.scalar.copy)
         quantize_weight(("g", 0), 0)
         part_words(2, 3, "staging_g00")
         quantize_weight(("g", 0), 1)
-        cast(("g", 1), 0, nc.scalar.copy)
-        cast(("g", 1), 1, nc.vector.tensor_copy)
+        round_weight(("g", 1), 0, nc.scalar.copy)
+        round_weight(("g", 1), 1, nc.vector.tensor_copy)
         quantize_weight(("g", 1), 1)
         quantize_weight(("g", 1), 0)
         part_words(3, 4, "staging_g10")
-        cast(("u", 0), 0, nc.vector.tensor_copy)
-        cast(("u", 0), 1, nc.vector.tensor_copy)
+        round_weight(("u", 0), 0, nc.vector.tensor_copy)
+        round_weight(("u", 0), 1, nc.vector.tensor_copy)
         quantize_weight(("u", 0), 0)
         quantize_weight(("u", 0), 1)
-        cast(("u", 1), 0, nc.vector.tensor_copy)
-        cast(("u", 1), 1, nc.vector.tensor_copy, 0, SHARE)
-        cast(("u", 1), 1, nc.scalar.copy, SHARE, R)
+        round_weight(("u", 1), 0, nc.vector.tensor_copy)
+        round_weight(("u", 1), 1, nc.vector.tensor_copy, 0, SHARE)
+        round_weight(("u", 1), 1, nc.scalar.copy, SHARE, R)
         quantize_weight(("u", 1), 0)
         quantize_weight(("u", 1), 1)
 
-        def new_bank(i):
-            return psum.tile([P, HALF], F32, name="bank%d" % i)
-
-        def token_major(bank):
-            return bank[:].rearrange("p (t j) -> p j t", t=PACK)
-
-        def chunk_of(tile, c):
-            return tile[:, c * CHUNK * PACK : (c + 1) * CHUNK * PACK].rearrange("p (j t) -> p j t", t=PACK)
-
-        late = keep.tile([P, 2, 2 * QUARTER * 2], F32, name="gate_late", tag="raw_u1")
+        late = shared.tile([P, 2, 2 * QUARTER * 2], F32, name="gate_late", align_bytes=64, offset=RAW_U1_AT)
         soon = keep.tile([P, 2, 2 * QUARTER * 2], F32, name="gate_soon")
         gate_pairs = (soon[:, 0], soon[:, 1], late[:, 0], late[:, 1])
         gate_order = ((1, 0), (1, 1), (0, 0), (0, 1), (1, 2), (0, 2), (1, 3), (0, 3))
@@ -209,7 +208,7 @@ def tile_list_gmlpt_tanh_res_none_kernel(
         def gate_tanh(u, q):
             dst = gate_pairs[q][:, u * QUARTER * 2 : (u + 1) * QUARTER * 2].rearrange("p (j e) -> p j e", e=2)
             src = gate_banks[u, q][:].rearrange("p (e j) -> p j e", e=2)
-            nc.scalar.activation(dst, src, TANH, bias=warm_out[:, 0:1])
+            nc.scalar.activation(dst, src, TANH, bias=gate_bias[:, 0:1])
 
         for u in range(2):
             for q in range(3):
@@ -225,9 +224,8 @@ def tile_list_gmlpt_tanh_res_none_kernel(
         hidden = keep.tile([P, J * PACK], BF16, name="hidden", align_bytes=64)
         h_codes = keep.tile([P, J], U32, name="h_codes", align_bytes=64)
         h_scales = keep.tile([P, J], U8, name="h_scales", align_bytes=64)
-        result = keep.tile([P, N // P, J], F32, name="result")
         out_rows = out.rearrange("(b p) j -> p b j", p=P)
-        wd_planes = wd_scales[:].bitcast(U8)
+        wd_scales = wd_planes[:].bitcast(U8)
 
         up_banks = {}
 
@@ -263,38 +261,42 @@ def tile_list_gmlpt_tanh_res_none_kernel(
             moving = dict(rhs=h_codes[:, j0 : j0 + width].bitcast(FP8X4), rhs_scale=h_scales[:, j0 : j0 + width])
             nc.tensor.matmul_mx(
                 out=acc,
-                lhsT=wd4_codes[:].bitcast(U8)[:, 2 * b * P : 2 * (b + 1) * P].bitcast(FP4X4),
-                lhsT_scale=wd_planes[:, 0, b * P : (b + 1) * P],
+                lhsT=wd8_codes[:, b * P : (b + 1) * P].bitcast(FP8X4),
+                lhsT_scale=wd_scales[:, N + b * P : N + (b + 1) * P],
                 start=True,
                 stop=False,
                 **moving
             )
             nc.tensor.matmul_mx(
                 out=acc,
-                lhsT=wd8_codes[:, b * P : (b + 1) * P].bitcast(FP8X4),
-                lhsT_scale=wd_planes[:, 1, b * P : (b + 1) * P],
+                lhsT=wd4_codes.bitcast(U8)[:, 2 * b * P : 2 * (b + 1) * P].bitcast(FP4X4),
+                lhsT_scale=wd_scales[:, b * P : (b + 1) * P],
                 start=False,
                 stop=True,
                 **moving
             )
 
-        def store(b0, b1, j0, width):
-            nc.sync.dma_start(out_rows[:, b0:b1, j0 : j0 + width], result[:, b0:b1, j0 : j0 + width])
+        def new_result(name, blocks, width):
+            return keep.tile([P, blocks, width], F32, name=name)
 
-        def down_chunk(c, i, copy):
-            j0 = c * CHUNK
+        def store(result, b0, j0):
+            blocks, width = result.shape[1:]
+            nc.sync.dma_start(out_rows[:, b0 : b0 + blocks, j0 : j0 + width], result[:])
+
+        def down_chunk(c, i, copy, dst):
             bank = new_bank(i)
             for b in range(N // P):
-                down_group(bank[:, b * CHUNK : (b + 1) * CHUNK], b, j0, CHUNK)
-            copy(result[:, :, j0 : j0 + CHUNK], bank[:, 0 : 2 * CHUNK].rearrange("p (b j) -> p b j", b=N // P))
+                down_group(bank[:, b * CHUNK : (b + 1) * CHUNK], b, c * CHUNK, CHUNK)
+            copy(dst, bank[:, 0 : 2 * CHUNK].rearrange("p (b j) -> p b j", b=N // P))
 
         def down_pair(c, banks):
             j0 = c * CHUNK
             for b in range(N // P):
                 bank = new_bank(banks[b])
                 down_group(bank[:, 0 : 2 * CHUNK], b, j0, 2 * CHUNK)
-                nc.scalar.copy(result[:, b, j0 : j0 + 2 * CHUNK], bank[:, 0 : 2 * CHUNK])
-                store(b, b + 1, j0, 2 * CHUNK)
+                result = new_result("result%d_%d" % (c, b), 1, 2 * CHUNK)
+                nc.scalar.copy(result[:, 0], bank[:, 0 : 2 * CHUNK])
+                store(result, b, j0)
 
         early = (0, ASIDE, 1, 3)
         for i, c in enumerate(early):
@@ -310,36 +312,37 @@ def tile_list_gmlpt_tanh_res_none_kernel(
         for c in early[2:]:
             up_passes(c, 1, (2, 3, 0, 1), last=1)
         up_rows = keep.tile([P, CHUNK * PACK], F32, name="up_rows")
-        nc.scalar.copy(chunk_of(up_rows, 0), token_major(up_banks[ASIDE]))
+        nc.scalar.copy(
+            up_rows[:].rearrange("p (j t) -> p j t", t=PACK), up_banks[ASIDE][:].rearrange("p (t j) -> p j t", t=PACK)
+        )
         nc.gpsimd.tensor_tensor(by_pairs(hidden, ASIDE), by_pairs(up_rows, 0), gate_of(ASIDE), MULT)
         for u, q in gate_order[6:]:
             gate_tanh(u, q)
-        up_both(4, 4)
-        up_both(5, 5)
-        up_both(6, 6)
-        up_both(7, 7)
-        multiply(0)
-        multiply(1)
-        multiply(3)
-        multiply(4)
+        for c in range(4, 8):
+            up_both(c, c)
+        for c in (0, 1, 3, 4):
+            multiply(c)
         quantize_hidden(0, 2 * CHUNK)
         down_pair(0, (0, 1))
         multiply(5)
         quantize_hidden(2 * CHUNK, 2 * CHUNK)
         down_pair(2, (2, 3))
         quantize_hidden(4 * CHUNK, CHUNK)
-        down_chunk(4, 4, nc.scalar.copy)
+        result45 = new_result("result45", 2, 2 * CHUNK)
+        down_chunk(4, 4, nc.scalar.copy, result45[:, :, 0:CHUNK])
         multiply(6)
         quantize_hidden(5 * CHUNK, CHUNK)
-        down_chunk(5, 5, nc.scalar.copy)
-        store(0, 2, 4 * CHUNK, 2 * CHUNK)
+        down_chunk(5, 5, nc.scalar.copy, result45[:, :, CHUNK:])
+        store(result45, 0, 4 * CHUNK)
         multiply(7)
         quantize_hidden(6 * CHUNK, CHUNK)
         quantize_hidden(7 * CHUNK, CHUNK)
-        down_chunk(6, 0, nc.vector.tensor_copy)
-        store(0, 2, 6 * CHUNK, CHUNK)
+        result6 = new_result("result6", 2, CHUNK)
+        down_chunk(6, 0, nc.vector.tensor_copy, result6[:])
+        store(result6, 0, 6 * CHUNK)
+        result7 = new_result("result7", 2, CHUNK)
         for b, i in enumerate((1, 6)):
             bank = new_bank(i)
             down_group(bank[:, 0:CHUNK], b, 7 * CHUNK, CHUNK)
-            nc.scalar.copy(result[:, b, 7 * CHUNK : J], bank[:, 0:CHUNK])
-        store(0, 2, 7 * CHUNK, CHUNK)
+            nc.scalar.copy(result7[:, b], bank[:, 0:CHUNK])
+        store(result7, 0, 7 * CHUNK)

@@ -27,12 +27,8 @@ CHUNK = 128
 ROW0 = 96
 ASIDE = 2
 SHARE = 160
-RAW_BYTES = PACK * R * 4
 EARLY_PLANE_BYTES = 128
-RAW_G1_AT = EARLY_PLANE_BYTES
-RAW_U0_AT = RAW_G1_AT + RAW_BYTES
-RAW_U1_AT = RAW_U0_AT + RAW_BYTES
-WORD_WINDOW_AT = RAW_U1_AT - 64
+RAW_U1_AT = T
 
 
 def tile_list_gmlpt_tanh_res_none_kernel(
@@ -46,7 +42,7 @@ def tile_list_gmlpt_tanh_res_none_kernel(
 
         offsets = keep.tile([P, J // 16], U16, name="offsets")
         scale_window = shared.tile([P, T // 4], I32, name="scale_window", align_bytes=64, offset=0)
-        word_window = shared.tile([P, T], I32, name="word_window", align_bytes=64, offset=WORD_WINDOW_AT)
+        word_window = keep.tile([P, T], I32, name="word_window", align_bytes=64)
         picked_scales = keep.tile([P, J // 4], I32, name="picked_scales", align_bytes=64)
         picked_words = keep.tile([P, J], I32, name="picked_words", align_bytes=64)
         v_planes = keep.tile([P, PASSES * J // 4], I32, name="v_planes", align_bytes=64)
@@ -57,8 +53,8 @@ def tile_list_gmlpt_tanh_res_none_kernel(
         zero_column = keep.tile([P, 8], F32, name="zero_column")
         gate_bias = keep.tile([P, 8], F32, name="gate_bias")
 
-        nc.vector.memset(scale_window[0:ROW0, :], 0)
         nc.vector.memset(wd_planes[:], 0)
+        nc.vector.memset(scale_window[0:ROW0, :], 0)
         nc.vector.memset(wd_codes[:], 0)
         nc.vector.memset(v_planes[:], 0)
         nc.gpsimd.memset(zero_column[:], 0.0)
@@ -86,13 +82,14 @@ def tile_list_gmlpt_tanh_res_none_kernel(
         nc.sync.dma_start(scale_window[ROW0:P, :], tab_scales.bitcast(I32).rearrange("a q t -> (a q) t"))
         nc.sync.dma_start(offsets[:], offs)
         nc.sync.dma_start(word_window[:], tab_words[0].rearrange("p t b -> p (t b)").bitcast(I32))
+        load_down_scales(0, wd4_scales, (0, 1, 2))
         load_weight("g", wg, 0, keep)
-        load_down_scales(0, wd4_scales, (0,))
+        load_down_scales(0, wd4_scales, (3,))
         nc.vector.tensor_copy(picked_scales[:].bitcast(U8), scale_window[:].bitcast(U8).indirect(offsets[:]))
         early_plane = shared.tile([P, EARLY_PLANE_BYTES // 4], U32, name="early_plane", align_bytes=64, offset=0)
         nc.scalar.copy(early_plane[:], wd8_codes[:, 0 : EARLY_PLANE_BYTES // 4].bitcast(U32))
         move_scales(0)
-        load_weight("g", wg, 1, shared, align_bytes=64, offset=RAW_G1_AT)
+        load_weight("g", wg, 1, keep)
         move_scales(1)
 
         def gather_words(h):
@@ -101,10 +98,10 @@ def tile_list_gmlpt_tanh_res_none_kernel(
                 word_window[:].bitcast(U32).indirect(offsets[:, h * HALF // 16 : (h + 1) * HALF // 16]),
             )
 
+        load_weight("u", wu, 0, keep)
+        load_weight("u", wu, 1, shared, align_bytes=64, offset=RAW_U1_AT)
         gather_words(0)
         gather_words(1)
-        load_weight("u", wu, 0, shared, align_bytes=64, offset=RAW_U0_AT)
-        load_weight("u", wu, 1, shared, align_bytes=64, offset=RAW_U1_AT)
 
         def new_bank(i):
             return psum.tile([P, BANK], F32, name="bank%d" % i)
@@ -127,7 +124,6 @@ def tile_list_gmlpt_tanh_res_none_kernel(
 
         nc.sync.dma_start(wd4_codes, wd4_words[0].bitcast(I32))
         nc.sync.dma_start(wd8_codes, wd8_words[0].rearrange("p n b -> p (n b)").bitcast(I32))
-        load_down_scales(0, wd4_scales, (1, 2, 3))
         load_down_scales(1, wd8_scales, range(4))
 
         grouped, w_codes, w_scales, v_codes = {}, {}, {}, {}
@@ -261,16 +257,16 @@ def tile_list_gmlpt_tanh_res_none_kernel(
             moving = dict(rhs=h_codes[:, j0 : j0 + width].bitcast(FP8X4), rhs_scale=h_scales[:, j0 : j0 + width])
             nc.tensor.matmul_mx(
                 out=acc,
-                lhsT=wd8_codes[:, b * P : (b + 1) * P].bitcast(FP8X4),
-                lhsT_scale=wd_scales[:, N + b * P : N + (b + 1) * P],
+                lhsT=wd4_codes.bitcast(U8)[:, 2 * b * P : 2 * (b + 1) * P].bitcast(FP4X4),
+                lhsT_scale=wd_scales[:, b * P : (b + 1) * P],
                 start=True,
                 stop=False,
                 **moving
             )
             nc.tensor.matmul_mx(
                 out=acc,
-                lhsT=wd4_codes.bitcast(U8)[:, 2 * b * P : 2 * (b + 1) * P].bitcast(FP4X4),
-                lhsT_scale=wd_scales[:, b * P : (b + 1) * P],
+                lhsT=wd8_codes[:, b * P : (b + 1) * P].bitcast(FP8X4),
+                lhsT_scale=wd_scales[:, N + b * P : N + (b + 1) * P],
                 start=False,
                 stop=True,
                 **moving

@@ -29,6 +29,7 @@ ASIDE = 2
 SHARE = 160
 EARLY_PLANE_BYTES = 128
 RAW_U1_AT = T
+BURST = 256
 
 
 def tile_list_gmlpt_tanh_res_none_kernel(
@@ -38,11 +39,12 @@ def tile_list_gmlpt_tanh_res_none_kernel(
     with ExitStack() as ctx:
         keep = ctx.enter_context(tc.tile_pool(name="keep", bufs=1))
         shared = ctx.enter_context(tc.tile_pool(name="shared", bufs=1))
+        wide = ctx.enter_context(tc.tile_pool(name="wide", bufs=1))
         psum = ctx.enter_context(tc.psum_pool(name="psum", bufs=1))
 
         offsets = keep.tile([P, J // 16], U16, name="offsets")
-        scale_window = shared.tile([P, T // 4], I32, name="scale_window", align_bytes=64, offset=0)
-        word_window = keep.tile([P, T], I32, name="word_window", align_bytes=64)
+        scale_window = shared.tile([P, T // 4], I32, name="scale_window", align_bytes=BURST, offset=0)
+        word_window = wide.tile([P, T], I32, name="word_window", align_bytes=BURST)
         picked_scales = keep.tile([P, J // 4], I32, name="picked_scales", align_bytes=64)
         picked_words = keep.tile([P, J], I32, name="picked_words", align_bytes=64)
         v_planes = keep.tile([P, PASSES * J // 4], I32, name="v_planes", align_bytes=64)
@@ -83,13 +85,13 @@ def tile_list_gmlpt_tanh_res_none_kernel(
         nc.sync.dma_start(offsets[:], offs)
         nc.sync.dma_start(word_window[:], tab_words[0].rearrange("p t b -> p (t b)").bitcast(I32))
         load_down_scales(0, wd4_scales, (0, 1, 2))
-        load_weight("g", wg, 0, keep)
+        load_weight("g", wg, 0, wide, align_bytes=BURST)
         load_down_scales(0, wd4_scales, (3,))
         nc.vector.tensor_copy(picked_scales[:].bitcast(U8), scale_window[:].bitcast(U8).indirect(offsets[:]))
-        early_plane = shared.tile([P, EARLY_PLANE_BYTES // 4], U32, name="early_plane", align_bytes=64, offset=0)
+        early_plane = shared.tile([P, EARLY_PLANE_BYTES // 4], U32, name="early_plane", align_bytes=BURST, offset=0)
         nc.scalar.copy(early_plane[:], wd8_codes[:, 0 : EARLY_PLANE_BYTES // 4].bitcast(U32))
         move_scales(0)
-        load_weight("g", wg, 1, keep)
+        load_weight("g", wg, 1, wide, align_bytes=BURST)
         move_scales(1)
 
         def gather_words(h):
@@ -98,8 +100,8 @@ def tile_list_gmlpt_tanh_res_none_kernel(
                 word_window[:].bitcast(U32).indirect(offsets[:, h * HALF // 16 : (h + 1) * HALF // 16]),
             )
 
-        load_weight("u", wu, 0, keep)
-        load_weight("u", wu, 1, shared, align_bytes=64, offset=RAW_U1_AT)
+        load_weight("u", wu, 0, wide, align_bytes=BURST)
+        load_weight("u", wu, 1, shared, align_bytes=BURST, offset=RAW_U1_AT)
         gather_words(0)
         gather_words(1)
 
@@ -190,7 +192,7 @@ def tile_list_gmlpt_tanh_res_none_kernel(
         quantize_weight(("u", 1), 0)
         quantize_weight(("u", 1), 1)
 
-        late = shared.tile([P, 2, 2 * QUARTER * 2], F32, name="gate_late", align_bytes=64, offset=RAW_U1_AT)
+        late = shared.tile([P, 2, 2 * QUARTER * 2], F32, name="gate_late", align_bytes=BURST, offset=RAW_U1_AT)
         soon = keep.tile([P, 2, 2 * QUARTER * 2], F32, name="gate_soon")
         gate_pairs = (soon[:, 0], soon[:, 1], late[:, 0], late[:, 1])
         gate_order = ((1, 0), (1, 1), (0, 0), (0, 1), (1, 2), (0, 2), (1, 3), (0, 3))
@@ -273,7 +275,7 @@ def tile_list_gmlpt_tanh_res_none_kernel(
             )
 
         def new_result(name, blocks, width):
-            return keep.tile([P, blocks, width], F32, name=name)
+            return wide.tile([P, blocks, width], F32, name=name, align_bytes=BURST)
 
         def store(result, b0, j0):
             blocks, width = result.shape[1:]

@@ -30,6 +30,7 @@ SHARE = 160
 EARLY_PLANE_BYTES = 128
 RAW_U1_AT = T
 BURST = 256
+STATIONARY_PLANE_AT, MOVING_AT, MOVING_PLANE_AT = 64, 128, 192
 
 
 def tile_list_gmlpt_tanh_res_none_kernel(
@@ -47,18 +48,23 @@ def tile_list_gmlpt_tanh_res_none_kernel(
         word_window = wide.tile([P, T], I32, name="word_window", align_bytes=BURST)
         picked_scales = keep.tile([P, J // 4], I32, name="picked_scales", align_bytes=64)
         picked_words = keep.tile([P, J], I32, name="picked_words", align_bytes=64)
-        v_planes = keep.tile([P, PASSES * J // 4], I32, name="v_planes", align_bytes=64)
-        wd_codes = keep.tile([P, N + N // 2], I32, name="wd_codes", align_bytes=64)
+
+        def placed(name, columns, dtype, size, at, tag=None):
+            tile = keep.tile([P, columns + at // size], dtype, name=name, tag=tag or name, align_bytes=BURST)
+            return tile[:, at // size :]
+
+        v_planes = placed("v_planes", PASSES * J // 4, I32, 4, MOVING_PLANE_AT)
+        wd_codes = placed("wd_codes", N + N // 2, I32, 4, 0)
         wd8_codes = wd_codes[:, 0:N]
         wd4_codes = wd_codes[:, N : N + N // 2]
-        wd_planes = keep.tile([P, N // 2], I32, name="wd_planes", align_bytes=64)
+        wd_planes = placed("wd_planes", N // 2, I32, 4, STATIONARY_PLANE_AT)
         zero_column = keep.tile([P, 8], F32, name="zero_column")
         gate_bias = keep.tile([P, 8], F32, name="gate_bias")
 
-        nc.vector.memset(wd_planes[:], 0)
+        nc.vector.memset(wd_planes, 0)
         nc.vector.memset(scale_window[0:ROW0, :], 0)
-        nc.vector.memset(wd_codes[:], 0)
-        nc.vector.memset(v_planes[:], 0)
+        nc.vector.memset(wd_codes, 0)
+        nc.vector.memset(v_planes, 0)
         nc.gpsimd.memset(zero_column[:], 0.0)
         nc.scalar.activation(gate_bias[:], zero_column[:], TANH)
 
@@ -111,7 +117,7 @@ def tile_list_gmlpt_tanh_res_none_kernel(
         idle_bank = new_bank(7)
         for stationary_plane, moving_plane in (
             (early_plane[:].bitcast(U8), wd4_codes.bitcast(U8)),
-            (wd4_codes.bitcast(U8)[:, 0:P], wd_planes[:].bitcast(U8)),
+            (wd4_codes.bitcast(U8)[:, 0:P], wd_planes.bitcast(U8)),
         ):
             for repeat in range(2):
                 nc.tensor.matmul_mx(
@@ -132,9 +138,9 @@ def tile_list_gmlpt_tanh_res_none_kernel(
         for key in raw:
             for u in range(2):
                 tag = "staging_%s%d%d" % (key[0], key[1], u)
-                grouped[key, u] = keep.tile([P, 2, P * PACK], BF16, name=tag, tag=tag, align_bytes=64)
-            w_codes[key] = keep.tile([P, R], U32, name="w_codes_%s%d" % key, align_bytes=64)
-            w_scales[key] = keep.tile([P, R], U8, name="w_scales_%s%d" % key, align_bytes=64)
+                grouped[key, u] = keep.tile([P, 2, P * PACK], BF16, name=tag, tag=tag, align_bytes=BURST)
+            w_codes[key] = placed("w_codes_%s%d" % key, R, U32, 4, 0)
+            w_scales[key] = placed("w_scales_%s%d" % key, R, U8, 1, STATIONARY_PLANE_AT)
 
         def round_weight(key, u, copy, c0=0, c1=R):
             src = raw[key][:, :, c0:c1].rearrange("p j (m u e) -> p u m j e", u=2, e=2)[:, u]
@@ -151,13 +157,13 @@ def tile_list_gmlpt_tanh_res_none_kernel(
 
         def part_words(q0, q1, tag):
             width = (q1 - q0) * QUARTER
-            parted = keep.tile([P, PASSES, 2 * width], U8, name="v_codes%d" % q0, tag=tag, align_bytes=64)
+            parted = placed("v_codes%d" % q0, PASSES * 2 * width, U8, 1, MOVING_AT, tag).rearrange("p (a x) -> p a x", a=PASSES)
             src = picked_words[:, q0 * QUARTER : q1 * QUARTER].bitcast(U16).rearrange("p (j d) -> p d j", d=2)
-            nc.vector.tensor_copy(parted[:].bitcast(U16), src)
+            nc.vector.tensor_copy(parted.bitcast(U16), src)
             for q in range(q0, q1):
                 v_codes[q] = parted[:, :, 2 * (q - q0) * QUARTER : 2 * (q - q0 + 1) * QUARTER]
 
-        v_scales = v_planes[:].bitcast(U8)
+        v_scales = v_planes.bitcast(U8)
 
         def first_layer_pass(acc, key, t, j0, width, start, stop):
             a = key[1]
@@ -220,10 +226,10 @@ def tile_list_gmlpt_tanh_res_none_kernel(
             gate_tanh(u, q)
 
         hidden = keep.tile([P, J * PACK], BF16, name="hidden", align_bytes=64)
-        h_codes = keep.tile([P, J], U32, name="h_codes", align_bytes=64)
-        h_scales = keep.tile([P, J], U8, name="h_scales", align_bytes=64)
+        h_codes = placed("h_codes", J, U32, 4, MOVING_AT)
+        h_scales = placed("h_scales", J, U8, 1, MOVING_PLANE_AT)
         out_rows = out.rearrange("(b p) j -> p b j", p=P)
-        wd_scales = wd_planes[:].bitcast(U8)
+        wd_scales = wd_planes.bitcast(U8)
 
         up_banks = {}
 

@@ -181,13 +181,12 @@ def tile_list_gmlpt_tanh_res_none_kernel(
         round_weight(("g", 0), 0, nc.scalar.copy)
         round_weight(("g", 0), 1, nc.scalar.copy)
         quantize_weight(("g", 0), 0)
-        part_words(2, 3, "staging_g00")
+        part_words(2, 4, "staging_g00")
         quantize_weight(("g", 0), 1)
         round_weight(("g", 1), 0, nc.scalar.copy)
         round_weight(("g", 1), 1, nc.vector.tensor_copy)
         quantize_weight(("g", 1), 1)
         quantize_weight(("g", 1), 0)
-        part_words(3, 4, "staging_g10")
         round_weight(("u", 0), 0, nc.vector.tensor_copy)
         round_weight(("u", 0), 1, nc.vector.tensor_copy)
         quantize_weight(("u", 0), 0)
@@ -215,13 +214,10 @@ def tile_list_gmlpt_tanh_res_none_kernel(
             nc.scalar.activation(dst, src, TANH, bias=gate_bias[:, 0:1])
 
         for u in range(2):
-            for q in range(3):
+            for q in range(4):
                 gate_passes(u, q, 0, True)
-        for u, q in gate_order[:6]:
+        for u, q in gate_order:
             gate_passes(u, q, 1, False)
-        for u, q in gate_order[6:]:
-            gate_passes(u, q, 1, True)
-            gate_passes(u, q, 0, False)
         for u, q in gate_order[:6]:
             gate_tanh(u, q)
 

from contextlib import ExitStack

import concourse.mybir as mybir

K, R, N, T, J = 1024, 512, 256, 2048, 1024
FLOPS = 2 * J * (2 * K * R + 2 * R * N)

F32 = mybir.dt.float32
BF16 = mybir.dt.bfloat16
I32 = mybir.dt.int32
U32 = mybir.dt.uint32
U16 = mybir.dt.uint16
U8 = mybir.dt.uint8
FP8X4 = mybir.dt.float8_e4m3fn_x4
FP4X4 = mybir.dt.float4_e2m1fn_x4
TANH = mybir.ActivationFunctionType.Tanh
MULT = mybir.AluOpType.mult

P = 128
PACK = 4
K_PASS = P * PACK
PASSES = K // K_PASS
BANK = 512
HALF = 512
QUARTER = 256
CHUNK = 128
ROW0 = 96
ASIDE = 2
SHARE = 160
EARLY_PLANE_BYTES = 128
RAW_U1_AT = T
BURST = 256
STATIONARY_PLANE_AT, MOVING_AT, MOVING_PLANE_AT = 64, 128, 192


def tile_list_gmlpt_tanh_res_none_kernel(
    tc, tab_words, tab_scales, wg, wu, wd4_words, wd4_scales, wd8_words, wd8_scales, offs, out
):
    nc = tc.nc
    with ExitStack() as ctx:
        keep = ctx.enter_context(tc.tile_pool(name="keep", bufs=1))
        shared = ctx.enter_context(tc.tile_pool(name="shared", bufs=1))
        wide = ctx.enter_context(tc.tile_pool(name="wide", bufs=1))
        psum = ctx.enter_context(tc.psum_pool(name="psum", bufs=1))

        offsets = keep.tile([P, J // 16], U16, name="offsets")
        scale_window = shared.tile([P, T // 4], I32, name="scale_window", align_bytes=BURST, offset=0)
        word_window = wide.tile([P, T], I32, name="word_window", align_bytes=BURST)
        picked_scales = keep.tile([P, J // 4], I32, name="picked_scales", align_bytes=64)
        picked_words = keep.tile([P, J], I32, name="picked_words", align_bytes=64)

        def placed(name, columns, dtype, size, at, tag=None):
            tile = keep.tile([P, columns + at // size], dtype, name=name, tag=tag or name, align_bytes=BURST)
            return tile[:, at // size :]

        v_planes = placed("v_planes", PASSES * J // 4, I32, 4, MOVING_PLANE_AT)
        wd_codes = placed("wd_codes", N + N // 2, I32, 4, 0)
        wd8_codes = wd_codes[:, 0:N]
        wd4_codes = wd_codes[:, N : N + N // 2]
        wd_planes = placed("wd_planes", N // 2, I32, 4, STATIONARY_PLANE_AT)
        zero_column = keep.tile([P, 8], F32, name="zero_column")
        gate_bias = keep.tile([P, 8], F32, name="gate_bias")

        nc.vector.memset(wd_planes, 0)
        nc.vector.memset(scale_window[0:ROW0, :], 0)
        nc.vector.memset(wd_codes, 0)
        nc.vector.memset(v_planes, 0)
        nc.gpsimd.memset(zero_column[:], 0.0)
        nc.scalar.activation(gate_bias[:], zero_column[:], TANH)

        raw = {}

        def load_weight(name, w, a, pool, **place):
            raw[name, a] = pool.tile([P, PACK, R], F32, name="raw_%s%d" % (name, a), **place)
            rows = w[a * K_PASS : (a + 1) * K_PASS, :].rearrange("(p j) c -> p j c", j=PACK)
            nc.sync.dma_start(raw[name, a][:], rows)

        def load_down_scales(f, scales, which):
            rows = scales[0].bitcast(I32).rearrange("(q r) n -> r q n", r=4)
            for r in which:
                nc.sync.dma_start(wd_planes[r:P:32, f * N // 4 : (f + 1) * N // 4], rows[r])

        def move_scales(a):
            first = ROW0 + 16 * a
            for r in range(4):
                nc.sync.dma_start(
                    v_planes[r:P:32, a * J // 4 : (a + 1) * J // 4], picked_scales[first + r : first + 16 : 4, :]
                )

        nc.sync.dma_start(scale_window[ROW0:P, :], tab_scales.bitcast(I32).rearrange("a q t -> (a q) t"))
        nc.sync.dma_start(offsets[:], offs)
        nc.sync.dma_start(word_window[:], tab_words[0].rearrange("p t b -> p (t b)").bitcast(I32))
        load_down_scales(0, wd4_scales, (0, 1, 2))
        load_weight("g", wg, 0, wide, align_bytes=BURST)
        load_down_scales(0, wd4_scales, (3,))
        nc.vector.tensor_copy(picked_scales[:].bitcast(U8), scale_window[:].bitcast(U8).indirect(offsets[:]))
        early_plane = shared.tile([P, EARLY_PLANE_BYTES // 4], U32, name="early_plane", align_bytes=BURST, offset=0)
        nc.scalar.copy(early_plane[:], wd8_codes[:, 0 : EARLY_PLANE_BYTES // 4].bitcast(U32))
        move_scales(0)
        load_weight("g", wg, 1, wide, align_bytes=BURST)
        move_scales(1)

        def gather_words(h):
            nc.vector.tensor_copy(
                picked_words[:, h * HALF : (h + 1) * HALF].bitcast(U32),
                word_window[:].bitcast(U32).indirect(offsets[:, h * HALF // 16 : (h + 1) * HALF // 16]),
            )

        load_weight("u", wu, 0, wide, align_bytes=BURST)
        load_weight("u", wu, 1, shared, align_bytes=BURST, offset=RAW_U1_AT)
        gather_words(0)
        gather_words(1)

        def new_bank(i):
            return psum.tile([P, BANK], F32, name="bank%d" % i)

        idle_bank = new_bank(7)
        for stationary_plane, moving_plane in (
            (early_plane[:].bitcast(U8), wd4_codes.bitcast(U8)),
            (wd4_codes.bitcast(U8)[:, 0:P], wd_planes.bitcast(U8)),
        ):
            for repeat in range(2):
                nc.tensor.matmul_mx(
                    out=idle_bank[:],
                    lhsT=wd8_codes[:, 0:P].bitcast(FP8X4),
                    lhsT_scale=stationary_plane,
                    rhs=wd8_codes.bitcast(U8).bitcast(FP4X4),
                    rhs_scale=moving_plane,
                    start=True,
                    stop=True,
                )

        nc.sync.dma_start(wd4_codes, wd4_words[0].bitcast(I32))
        nc.sync.dma_start(wd8_codes, wd8_words[0].rearrange("p n b -> p (n b)").bitcast(I32))
        load_down_scales(1, wd8_scales, range(4))

        grouped, w_codes, w_scales, v_codes = {}, {}, {}, {}
        for key in raw:
            for u in range(2):
                tag = "staging_%s%d%d" % (key[0], key[1], u)
                grouped[key, u] = keep.tile([P, 2, P * PACK], BF16, name=tag, tag=tag, align_bytes=BURST)
            w_codes[key] = placed("w_codes_%s%d" % key, R, U32, 4, 0)
            w_scales[key] = placed("w_scales_%s%d" % key, R, U8, 1, STATIONARY_PLANE_AT)

        def round_weight(key, u, copy, c0=0, c1=R):
            src = raw[key][:, :, c0:c1].rearrange("p j (m u e) -> p u m j e", u=2, e=2)[:, u]
            dst = grouped[key, u][:, :, c0:c1].rearrange("p e (m j) -> p m j e", j=PACK)
            copy(dst, src)

        def quantize_weight(key, u):
            cols = slice(2 * u * P, 2 * (u + 1) * P)
            nc.vector.quantize_mx(
                out=w_codes[key][:, cols].bitcast(FP8X4),
                scales=w_scales[key][:, cols],
                in_=grouped[key, u][:].rearrange("p e x -> p (e x)"),
            )

        def part_words(q0, q1, tag):
            width = (q1 - q0) * QUARTER
            parted = placed("v_codes%d" % q0, PASSES * 2 * width, U8, 1, MOVING_AT, tag).rearrange("p (a x) -> p a x", a=PASSES)
            src = picked_words[:, q0 * QUARTER : q1 * QUARTER].bitcast(U16).rearrange("p (j d) -> p d j", d=2)
            nc.vector.tensor_copy(parted.bitcast(U16), src)
            for q in range(q0, q1):
                v_codes[q] = parted[:, :, 2 * (q - q0) * QUARTER : 2 * (q - q0 + 1) * QUARTER]

        v_scales = v_planes.bitcast(U8)

        def first_layer_pass(acc, key, t, j0, width, start, stop):
            a = key[1]
            nc.tensor.matmul_mx(
                out=acc,
                lhsT=w_codes[key][:, t * P : (t + 1) * P].bitcast(FP8X4),
                lhsT_scale=w_scales[key][:, t * P : (t + 1) * P],
                rhs=v_codes[j0 // QUARTER][:, a, 2 * (j0 % QUARTER) : 2 * (j0 % QUARTER + width)].bitcast(FP4X4),
                rhs_scale=v_scales[:, a * J + j0 : a * J + j0 + width],
                start=start,
                stop=stop,
            )

        part_words(0, 2, "v_codes0")
        round_weight(("g", 0), 0, nc.scalar.copy)
        round_weight(("g", 0), 1, nc.scalar.copy)
        quantize_weight(("g", 0), 0)
        part_words(2, 4, "staging_g00")
        quantize_weight(("g", 0), 1)
        round_weight(("g", 1), 0, nc.scalar.copy)
        round_weight(("g", 1), 1, nc.vector.tensor_copy)
        quantize_weight(("g", 1), 1)
        quantize_weight(("g", 1), 0)
        round_weight(("u", 0), 0, nc.vector.tensor_copy)
        round_weight(("u", 0), 1, nc.vector.tensor_copy)
        quantize_weight(("u", 0), 0)
        quantize_weight(("u", 0), 1)
        round_weight(("u", 1), 0, nc.vector.tensor_copy)
        round_weight(("u", 1), 1, nc.vector.tensor_copy, 0, SHARE)
        round_weight(("u", 1), 1, nc.scalar.copy, SHARE, R)
        quantize_weight(("u", 1), 0)
        quantize_weight(("u", 1), 1)

        late = shared.tile([P, 2, 2 * QUARTER * 2], F32, name="gate_late", align_bytes=BURST, offset=RAW_U1_AT)
        soon = keep.tile([P, 2, 2 * QUARTER * 2], F32, name="gate_soon")
        gate_pairs = (soon[:, 0], soon[:, 1], late[:, 0], late[:, 1])
        gate_order = ((1, 0), (1, 1), (0, 0), (0, 1), (1, 2), (0, 2), (1, 3), (0, 3))
        gate_banks = {key: new_bank(i) for i, key in enumerate(gate_order)}

        def gate_passes(u, q, a, opens):
            for e in range(2):
                acc = gate_banks[u, q][:, e * QUARTER : (e + 1) * QUARTER]
                first_layer_pass(acc, ("g", a), 2 * u + e, q * QUARTER, QUARTER, opens and e == 0, not opens and e == 1)

        def gate_tanh(u, q):
            dst = gate_pairs[q][:, u * QUARTER * 2 : (u + 1) * QUARTER * 2].rearrange("p (j e) -> p j e", e=2)
            src = gate_banks[u, q][:].rearrange("p (e j) -> p j e", e=2)
            nc.scalar.activation(dst, src, TANH, bias=gate_bias[:, 0:1])

        for u in range(2):
            for q in range(4):
                gate_passes(u, q, 0, True)
        for u, q in gate_order:
            gate_passes(u, q, 1, False)
        for u, q in gate_order[:6]:
            gate_tanh(u, q)

        hidden = keep.tile([P, J * PACK], BF16, name="hidden", align_bytes=64)
        h_codes = placed("h_codes", J, U32, 4, MOVING_AT)
        h_scales = placed("h_scales", J, U8, 1, MOVING_PLANE_AT)
        out_rows = out.rearrange("(b p) j -> p b j", p=P)
        wd_scales = wd_planes.bitcast(U8)

        up_banks = {}

        def up_passes(c, a, tiles, first=None, last=None):
            for t in tiles:
                acc = up_banks[c][:, t * CHUNK : (t + 1) * CHUNK]
                first_layer_pass(acc, ("u", a), t, c * CHUNK, CHUNK, t == first, t == last)

        def up_both(c, i):
            up_banks[c] = new_bank(i)
            up_passes(c, 1, (2, 3, 0, 1), first=2)
            up_passes(c, 0, (0, 1, 2, 3), last=3)

        def by_pairs(tile, c):
            return tile[:, c * CHUNK * PACK : (c + 1) * CHUNK * PACK].rearrange("p (j u e) -> p j u e", u=2, e=2)

        def gate_of(c):
            j0 = (c % 2) * CHUNK
            return gate_pairs[c // 2].rearrange("p (u j e) -> p j u e", u=2, e=2)[:, j0 : j0 + CHUNK]

        def multiply(c):
            src = up_banks[c][:].rearrange("p (u e j) -> p j u e", u=2, e=2)
            nc.vector.tensor_tensor(by_pairs(hidden, c), src, gate_of(c), MULT)

        def quantize_hidden(j0, width):
            nc.vector.quantize_mx(
                out=h_codes[:, j0 : j0 + width].bitcast(FP8X4),
                scales=h_scales[:, j0 : j0 + width],
                in_=hidden[:, j0 * PACK : (j0 + width) * PACK],
            )

        def down_group(acc, b, j0, width):
            moving = dict(rhs=h_codes[:, j0 : j0 + width].bitcast(FP8X4), rhs_scale=h_scales[:, j0 : j0 + width])
            nc.tensor.matmul_mx(
                out=acc,
                lhsT=wd4_codes.bitcast(U8)[:, 2 * b * P : 2 * (b + 1) * P].bitcast(FP4X4),
                lhsT_scale=wd_scales[:, b * P : (b + 1) * P],
                start=True,
                stop=False,
                **moving
            )
            nc.tensor.matmul_mx(
                out=acc,
                lhsT=wd8_codes[:, b * P : (b + 1) * P].bitcast(FP8X4),
                lhsT_scale=wd_scales[:, N + b * P : N + (b + 1) * P],
                start=False,
                stop=True,
                **moving
            )

        def new_result(name, blocks, width):
            return wide.tile([P, blocks, width], F32, name=name, align_bytes=BURST)

        def store(result, b0, j0):
            blocks, width = result.shape[1:]
            nc.sync.dma_start(out_rows[:, b0 : b0 + blocks, j0 : j0 + width], result[:])

        def down_chunk(c, i, copy, dst):
            bank = new_bank(i)
            for b in range(N // P):
                down_group(bank[:, b * CHUNK : (b + 1) * CHUNK], b, c * CHUNK, CHUNK)
            copy(dst, bank[:, 0 : 2 * CHUNK].rearrange("p (b j) -> p b j", b=N // P))

        def down_pair(c, banks):
            j0 = c * CHUNK
            for b in range(N // P):
                bank = new_bank(banks[b])
                down_group(bank[:, 0 : 2 * CHUNK], b, j0, 2 * CHUNK)
                result = new_result("result%d_%d" % (c, b), 1, 2 * CHUNK)
                nc.scalar.copy(result[:, 0], bank[:, 0 : 2 * CHUNK])
                store(result, b, j0)

        early = (0, ASIDE, 1, 3)
        for i, c in enumerate(early):
            up_banks[c] = new_bank(i)
        for tiles in ((0, 1), (2, 3)):
            for c in early[:2]:
                up_passes(c, 0, tiles, first=0)
        for c in early[2:]:
            up_passes(c, 0, (0, 1, 2, 3), first=0)
        for tiles in ((0, 1), (2, 3)):
            for c in early[:2]:
                up_passes(c, 1, tiles, last=3)
        for c in early[2:]:
            up_passes(c, 1, (2, 3, 0, 1), last=1)
        up_rows = keep.tile([P, CHUNK * PACK], F32, name="up_rows")
        nc.scalar.copy(
            up_rows[:].rearrange("p (j t) -> p j t", t=PACK), up_banks[ASIDE][:].rearrange("p (t j) -> p j t", t=PACK)
        )
        nc.gpsimd.tensor_tensor(by_pairs(hidden, ASIDE), by_pairs(up_rows, 0), gate_of(ASIDE), MULT)
        for u, q in gate_order[6:]:
            gate_tanh(u, q)
        for c in range(4, 8):
            up_both(c, c)
        for c in (0, 1, 3, 4):
            multiply(c)
        quantize_hidden(0, 2 * CHUNK)
        down_pair(0, (0, 1))
        multiply(5)
        quantize_hidden(2 * CHUNK, 2 * CHUNK)
        down_pair(2, (2, 3))
        quantize_hidden(4 * CHUNK, CHUNK)
        result45 = new_result("result45", 2, 2 * CHUNK)
        down_chunk(4, 4, nc.scalar.copy, result45[:, :, 0:CHUNK])
        multiply(6)
        quantize_hidden(5 * CHUNK, CHUNK)
        down_chunk(5, 5, nc.scalar.copy, result45[:, :, CHUNK:])
        store(result45, 0, 4 * CHUNK)
        multiply(7)
        quantize_hidden(6 * CHUNK, CHUNK)
        quantize_hidden(7 * CHUNK, CHUNK)
        result6 = new_result("result6", 2, CHUNK)
        down_chunk(6, 0, nc.vector.tensor_copy, result6[:])
        store(result6, 0, 6 * CHUNK)
        result7 = new_result("result7", 2, CHUNK)
        for b, i in enumerate((1, 6)):
            bank = new_bank(i)
            down_group(bank[:, 0:CHUNK], b, 7 * CHUNK, CHUNK)
            nc.scalar.copy(result7[:, b], bank[:, 0:CHUNK])
        store(result7, 0, 7 * CHUNK)
